import numpy as np, ml_dtypes
CORES = [40,64,80,88,96,104,120,144]
N = 8
BF = ml_dtypes.bfloat16
def f(rng, *shape):
    return (rng.standard_normal(shape, dtype=np.float32) * np.exp2(rng.integers(-2, 3, shape[:-1] + (1,)))).astype(BF)
def wide(rng, *shape):
    v = f(rng, *shape).astype(np.float32); k = shape[:-2] + (1, shape[-1])
    return (v * np.exp2(rng.integers(-6, 7, k)) * (rng.random(k) > 0.0625)).astype(BF)
P, NT, W, D = 1024, 64, 256, 64
def order(g):
    return range(N)
def places(ln):
    n = np.asarray(ln).reshape(-1, NT).astype(np.int64) + 1; m = len(n)
    t = np.repeat(np.tile(np.arange(NT), m), n.reshape(-1)).reshape(m, P)
    last = np.zeros((m, P), bool); last[np.arange(m)[:, None], np.add.accumulate(n, 1) - 1] = True
    return t, last
def steps(ln, ds):
    t, last = places(ln); m = len(t); src = np.arange(P) - np.take_along_axis(np.asarray(ds).reshape(m, NT).astype(np.int64), t, 1)
    e = np.zeros((m, P), np.int64); row = np.arange(m)
    for i in range(P):
        j = src[:, i]; e[:, i] = np.where(last[:, i], 0, 1 + np.where(j >= 0, e[row, np.maximum(j, 0)], 0))
    return e
def lengths(rng, at, big):
    n = np.zeros((N, 8, NT), np.int64)
    for r in range(N):
        for g in range(8):
            b = int(big[r, g]); rest = P - NT - b
            v = np.minimum(rng.multinomial(rest, rng.dirichlet(np.where(rng.random(NT - 1) < 0.25, 0.001, 1.0))), D)
            v = v + rng.multivariate_hypergeometric(D - v, rest - int(np.sum(v)))
            n[r, g] = np.insert(v, int(at[r, g]), b)
    return n
def starts(n):
    return np.add.accumulate(n + 1, 2) - n - 1
def distances(rng, n):
    s = starts(n); k = rng.integers(0, 4, n.shape)
    over = rng.integers(np.minimum(s, W - 1) + 1, W + 1)
    return np.where(k == 0, rng.integers(1, 9, n.shape), np.where(k == 3, over, rng.integers(1, W + 1, n.shape)))
def inside(rng, n, d, share):
    s = starts(n); d = np.array(d)
    for g in range(8):
        q = order(g)[0]; m = (d[q, g] > s[q, g]) & (s[q, g] > 0) & (rng.random(NT) < share)
        d[q, g] = np.where(m, rng.integers(1, np.maximum(s[q, g], 1) + 1), d[q, g])
    return d
def fit(n, d):
    d = np.array(d)
    for r in range(N):
        for g in range(8):
            e = []
            for t, (c, k) in enumerate(zip(n[r, g].tolist(), d[r, g].tolist())):
                s = len(e)
                for i in range(s, s + c): e.append(1 + (e[i - k] if i >= k else 0))
                if max(e[s:], default=0) > D:
                    d[r, g, t] = 1; e[s:] = range(1, c + 1)
                e.append(0)
    return d
def pack(rng, n, d):
    return {"ln": n.astype(np.int32), "ds": d.astype(np.int32), "le": f(rng, N, 128, NT)}
def setup_inputs(rng):
    n = lengths(rng, rng.integers(0, NT, (N, 8)), rng.integers(1, D + 1, (N, 8)))
    return pack(rng, n, fit(n, inside(rng, n, distances(rng, n), 0.75)))
def setup_inputs_deep(rng):
    at = np.where(rng.random((N, 8)) < 0.25, rng.choice(np.array([0, NT - 1]), (N, 8)), rng.integers(0, NT, (N, 8)))
    n = lengths(rng, at, np.full((N, 8), D)); d = np.where(rng.random(n.shape) < 0.5, rng.integers(1, 4, n.shape), distances(rng, n))
    d = inside(rng, n, d, 0.75); np.put_along_axis(d, at[:, :, None], 1, 2)
    return pack(rng, n, fit(n, d))
def setup_inputs_hops(rng):
    n = lengths(rng, rng.integers(0, NT, (N, 8)), rng.integers(1, D + 1, (N, 8)))
    return pack(rng, n, fit(n, inside(rng, n, rng.integers(W - 8, W + 1, n.shape), 1.0)))
def setup_inputs_ends(rng):
    at = rng.choice(np.array([0, NT - 1]), (N, 8)); at[:, :2] = 0
    n = lengths(rng, at, rng.integers(2, D + 1, (N, 8))); n[rng.integers(0, N)] = P // NT - 1
    s = starts(n); d = np.choose(rng.integers(0, 6, n.shape), [s * 0 + W, s * 0 + 1, s, s + 1, s + n, n])
    d = inside(rng, n, np.minimum(np.maximum(d, 1), W), 0.5); d[:, 0, 0] = W; d[:, 1, 0] = 1
    return pack(rng, n, fit(n, d))
def setup_inputs_long(rng):
    at = rng.integers(0, NT, (N, 8)); k = rng.integers(P // D, W + 1, (N, 8)); u = rng.integers(0, 3, (N, 8)); k = np.where(u == 0, P // D, np.where(u == 1, W, k))
    for g in range(8):
        q = order(g)[0]; at[q, g] = NT - 1; k[q, g] = rng.integers(P // D, min(W, NT - 1) + 1)
    n = np.zeros((N, 8, NT), np.int64); np.put_along_axis(n, at[:, :, None], P - NT, 2)
    d = rng.integers(1, W + 1, n.shape); np.put_along_axis(d, at[:, :, None], k[:, :, None], 2)
    return pack(rng, n, d)
def setup_inputs_spread(rng):
    d = setup_inputs(rng); d["le"] = wide(rng, N, 128, NT); return d
def check_inputs(d):
    bad = []; a = np.asarray(d["ln"]).astype(np.int64); b = np.asarray(d["ds"]).astype(np.int64)
    if (a < 0).any() or (np.sum(a, 2) + NT != P).any(): bad.append("lengths")
    if (b < 1).any() or (b > W).any(): bad.append("distances")
    if not bad and (steps(a, b) > D).any(): bad.append("steps")
    if not np.isfinite(np.asarray(d["le"]).astype(np.float32)).all(): bad.append("finite")
    return bad
def reference(ln, ds, le):
    y = np.zeros((N, 128, P), BF); t, last = places(ln); t = t.reshape(N, 8, P); last = last.reshape(N, 8, P)
    for g in range(8):
        buf = np.zeros((W + P, 16), BF)
        for r in order(g):
            a = np.ascontiguousarray(le[r, 16 * g:16 * g + 16].T); k = ds[r, g][t[r, g]].tolist(); tk = t[r, g].tolist(); own = last[r, g].tolist()
            for i in range(P):
                buf[W + i] = a[tk[i]] if own[i] else buf[W + i - k[i]]
            y[r, 16 * g:16 * g + 16] = buf[W:].T
            buf[:W] = buf[P:]
    return {"y": y}

@@ -1,0 +1,267 @@
+from concourse.bass import DstId, RemoteDMATransfer
+from concourse.mybir import AluOpType, ActivationFunctionType
+
+OFF = 2047
+BIG = 1344
+XA = 352
+XB = 672
+SCRATCH = {
+    "xl": ("sbuf", [8, 64], "int32"), "xd": ("sbuf", [8, 64], "int32"), "lm": ("sbuf", [8, 64], "int32"),
+    "lnf": ("sbuf", [8, 64], "float16"), "lastf": ("sbuf", [8, 64], "float16"), "dm": ("sbuf", [8, 64], "float16"),
+    "ei": ("sbuf", [8, 128], "int32"), "es": ("sbuf", [8, 128], "int32"), "ee": ("sbuf", [8, 128], "float16"),
+    "ui": ("sbuf", [128, 16], "int32"), "uu": ("sbuf", [128, 16], "int32"),
+    "ma": ("sbuf", [128, 16], "bfloat16"), "mb": ("sbuf", [128, 16], "bfloat16"), "mm": ("sbuf", [128, XB], "bfloat16"),
+    "av": ("sbuf", [128, 64], "bfloat16"), "bv": ("sbuf", [128, 64], "bfloat16"),
+    "A": ("sbuf", [128, 1056], "bfloat16"), "B": ("sbuf", [128, 1024], "bfloat16"),
+    "lsc": ("sbuf", [128, 64], "float32"), "lastw": ("sbuf", [128, 4], "uint16"),
+    "f16": ("sbuf", [128, 1024], "float16"), "r16": ("sbuf", [128, 1024], "float16"),
+    "FA": ("sbuf", [128, 1344], "float32"), "FB": ("sbuf", [128, 1344], "float32"),
+    "SC": ("sbuf", [128, 1024], "float32"),
+    "t16": ("sbuf", [128, 1024], "float16"), "q16": ("sbuf", [128, 1024], "float16"),
+    "L0": ("sbuf", [128, 64], "uint16"), "L1": ("sbuf", [128, 64], "uint16"),
+    "L2": ("sbuf", [128, 64], "uint16"), "L3": ("sbuf", [128, 64], "uint16"),
+    "LF": ("sbuf", [128, 64], "uint16"),
+    "hle": ("sbuf", [128, 64], "bfloat16"), "hli": ("sbuf", [128, 16], "uint16"),
+    "yb": ("sbuf", [128, 1024], "bfloat16"),
+    "ps1": ("psum", [128, 512], "float32"), "ps2": ("psum", [128, 512], "float32"),
+}
+for _k in range(8):
+    SCRATCH["V%d" % _k] = ("sbuf", [128, 320], "bfloat16")
+    SCRATCH["T%d" % _k] = ("sbuf", [128, 16], "uint16")
+SEMAPHORES = ["v", "s", "pe", "gi", "dln", "dds", "dle", "dy", "loc", "le", "hle", "hli"] + ["ar%d" % k for k in range(8)]
+
+
+def bits(engines):
+    return sum(1 << e for e in engines)
+
+
+def routes(rank, T, topo):
+    src = T.cores[rank]
+    later = list(range(len(T.cores) - 1, rank, -1))
+    straight = [r for r in later if topo.may_write(src, T.cores[r])]
+    cross = [r for r in later if r not in straight]
+    if not cross:
+        return straight, []
+    able = [h for h in topo.cores_of(src) if h != src and T.rank_of(h) is None and topo.may_write(h, T.cores[cross[0]])]
+    able.sort(key=lambda h: (topo.die(h) != topo.die(src), h))
+    n = min(2, len(cross), len(able))
+    eng = topo.engines(src, able[0])
+    w = len(eng) // n
+    return straight, [(able[i], cross[i::n], eng[i * w:(i + 1) * w]) for i in range(n)]
+
+
+def fan(g, T, topo, core, ranks, src, dst, rsem):
+    ids = []
+    for r in ranks:
+        rid, pid = topo.addr(T.cores[r], core)
+        ids.append(DstId(rid=rid, pnc=pid))
+    m = topo.mask(core, T.cores[ranks[0]])
+    g.remote_dma_fused([RemoteDMATransfer(dst_ids=ids, dma_engine_mask=m, remote_sem=rsem, srcs=[src],
+                                          dsts=[dst for _ in ranks])], local_sem=T.sem.loc)
+    return len(topo.engines(core, T.cores[ranks[0]]))
+
+
+def helper(g, core, T, topo):
+    for r in range(len(T.cores)):
+        if core not in topo.cores_of(T.cores[r]):
+            continue
+        for h, ranks, eng in routes(r, T, topo)[1]:
+            if h != core:
+                continue
+            n = 0
+            g.wait_ge(T.sem.hle, len(eng))
+            n += fan(g, T, topo, core, ranks, T.hle[:, :], T["V%d" % r][:, 0:64], T.sem.le)
+            g.wait_ge(T.sem.hli, len(eng))
+            for d in ranks:
+                n += fan(g, T, topo, core, [d], T.hli[:, :], T["T%d" % r][:, :], T.sem["ar%d" % r])
+            g.wait_ge(T.sem.loc, n)
+
+
+def rank_program(g, core, T, topo):
+    rank = T.rank_of(core)
+    if rank is None:
+        helper(g, core, T, topo)
+        return
+    op = AluOpType
+    fn = ActivationFunctionType
+    V, S, PE, SY = g.vector, g.scalar, g.tensor, g.sync
+    queue = {"v": V, "s": S, "pe": PE, "gi": g, "sy": SY}
+    cnt = {}
+    seen = {}
+
+    def need(q, toks):
+        top = {}
+        for sem, val in toks:
+            top[sem] = max(top.get(sem, 0), val)
+        for sem in top:
+            if seen.get((q, sem), 0) < top[sem]:
+                queue[q].wait_ge(T.sem[sem], top[sem])
+                seen[(q, sem)] = top[sem]
+
+    def done(sem, ins, n=1):
+        ins.then_inc(T.sem[sem], n)
+        cnt[sem] = cnt.get(sem, 0) + n
+        return (sem, cnt[sem])
+
+    def gath(q, out, win, lst, deps):
+        need(q, deps)
+        if q == "v":
+            return done("v", V.tensor_copy(out=out, in_=win.indirect(lst)))
+        return done("s", S.activation(out=out, in_=win.indirect(lst), func=fn.Copy))
+
+    def scan(out, data0, data1, initial, op0, op1, deps):
+        need("v", deps)
+        return done("v", V.tensor_tensor_scan(out=out, data0=data0, data1=data1, initial=initial, op0=op0, op1=op1))
+
+    def ts(out, in0, s1, s2, op0, op1, deps):
+        need("v", deps)
+        if op1 is None:
+            return done("v", V.tensor_scalar(out=out, in0=in0, scalar1=s1, scalar2=None, op0=op0))
+        return done("v", V.tensor_scalar(out=out, in0=in0, scalar1=s1, scalar2=s2, op0=op0, op1=op1))
+
+    mine = T["V%d" % rank]
+    ln = done("dln", SY.dma_start(out=T.xl[:, :], in_=T.ln[:, :]), 16)
+    ds = done("dds", S.dma_start(out=T.xd[:, :], in_=T.ds[:, :]), 16)
+    le = done("dle", SY.dma_start(out=mine[:, 0:64], in_=T.le[:, :]), 16)
+    ui = done("gi", g.iota(T.ui[:, :], [[1, 16]], 128, -1))
+    ei = done("gi", g.iota(T.ei[:, :], [[1, 128]], 0, -16))
+    b0 = done("gi", g.iota(T.B[:, :], [[0, 1024]], 0, 0, allow_small_or_imprecise_dtypes=True))
+    ida = done("gi", g.iota(T.FA[:, 0:320], [[1, 320]], -OFF, 0, allow_small_or_imprecise_dtypes=True))
+    idb = done("gi", g.iota(T.FB[:, 0:320], [[1, 320]], -OFF, 0, allow_small_or_imprecise_dtypes=True))
+    a1 = done("v", V.memset(T.A[:, :], 1.0))
+    av63 = done("v", V.memset(T.av[:, 63:64], 1.0))
+    uu = ts(T.uu[:, :], T.ui[:, :], 15, None, op.bitwise_and, None, [ui])
+    es = ts(T.es[:, :], T.ei[:, :], 4, None, op.arith_shift_right, None, [ei])
+    ma = ts(T.ma[:, :], T.uu[:, :], 0.0, -8192.0, op.is_equal, op.mult, [uu])
+    mb = ts(T.mb[:, :], T.uu[:, :], 1.0, float(BIG), op.is_equal, op.mult, [uu])
+    ee = ts(T.ee[:, :], T.es[:, :], 0.0, None, op.is_equal, None, [es])
+    need("v", [ma, mb])
+    mt = done("v", V.tensor_tensor(out=T.mm[:, 0:16], in0=T.ma[:, :], in1=T.mb[:, :], op=op.add))
+    w = 16
+    m64 = mt
+    while w < XB:
+        n = min(w, XB - w)
+        need("s", [mt])
+        mt = done("s", S.activation(out=T.mm[:, w:w + n], in_=T.mm[:, 0:n], func=fn.Copy))
+        w += n
+        if w == 64:
+            m64 = mt
+    last16 = T.mb[:, 0:1]
+
+    def relist(out, src, tmp, n, c0, add, deps):
+        t = scan(tmp, T.mm[:, 0:n], src, 0.0, op.add, op.max, deps + [mt if n > 64 else m64, mb])
+        return t
+
+    lnf = done("v", need("v", [ln]) or V.tensor_copy(out=T.lnf[:, :], in_=T.xl[:, :]))
+    lm = ts(T.lm[:, :], T.xl[:, :], 0, None, op.is_gt, None, [ln])
+    lastf = scan(T.lastf[:, :], T.A[0:8, 16:80], T.lnf[:, :], -1.0, op.add, op.add, [lnf, a1])
+    need("pe", [lastf, ee])
+    p1 = done("pe", PE.matmul(T.ps1[:, 0:64], T.ee[:, :], T.lastf[:, :], True, True))
+    need("v", [lm, ds])
+    dm = done("v", V.tensor_tensor(out=T.dm[:, :], in0=T.xd[:, :], in1=T.lm[:, :], op=op.mult))
+    need("pe", [dm])
+    p2 = done("pe", PE.matmul(T.ps2[:, 0:64], T.ee[:, :], T.dm[:, :], True, True))
+    need("s", [p2, av63, a1])
+    done("s", S.activation(out=T.av[:, 0:63], in_=T.ps2[:, 1:64], func=fn.Identity, bias=1.0, scale=-1.0))
+    done("s", S.activation(out=T.bv[:, :], in_=T.ps2[:, 0:64], func=fn.Copy))
+    vals = done("s", S.activation(out=T.A[:, 15:16], in_=T.ps2[:, 0:1], func=fn.Identity, bias=1.0, scale=-1.0))
+    t = relist(None, T.ps1[:, 0:64], T.lsc[:, :], 64, 0, 0, [p1])
+    lw = ts(T.lastw[:, :], T.lsc[:, 15:64:16], last16, -float(BIG), op.add, op.add, [t])
+    need("v", [lw, vals, b0])
+    done("v", V.tensor_copy(out=T.A[:, 16:1040].indirect(T.lastw[:, 0:4]), in_=T.av[:, :]))
+    sc2 = done("v", V.tensor_copy(out=T.B[:, 0:1024].indirect(T.lastw[:, 0:4]), in_=T.bv[:, :]))
+    h0 = scan(T.f16[:, 0:512], T.A[:, 15:527], T.B[:, 0:512], float(319 - OFF), op.add, op.add, [sc2])
+    need("s", [h0])
+    done("s", S.activation(out=T.FA[:, 320:832], in_=T.f16[:, 0:512], func=fn.Copy))
+    need("v", [h0])
+    hc = done("v", V.tensor_copy(out=T.lsc[:, 0:1], in_=T.f16[:, 511:512]))
+    h1 = scan(T.f16[:, 512:1024], T.A[:, 527:1039], T.B[:, 512:1024], T.lsc[:, 0:1], op.add, op.add, [hc])
+    need("s", [h1])
+    fcopy = done("s", S.activation(out=T.FA[:, 832:1344], in_=T.f16[:, 512:1024], func=fn.Copy))
+
+    add = float(OFF - BIG)
+    t = relist(None, T.f16[:, 0:512], T.r16[:, 0:512], 512, 0, 0, [h0])
+    la = ts(T.L0[:, 0:32], T.r16[:, 15:512:16], last16, add, op.add, op.add, [t])
+    t = relist(None, T.f16[:, 512:1024], T.r16[:, 512:1024], 512, 0, 0, [h1])
+    need("v", [fcopy, ida])
+    code = done("v", V.tensor_copy(out=T.FA[:, 320:1344].indirect(T.lastw[:, 0:4]), in_=T.FA[:, 0:64]))
+    lb = ts(T.L0[:, 32:64], T.r16[:, 527:1024:16], last16, add, op.add, op.add, [t])
+
+    FA, FB = T.FA[:, 0:1344], T.FB[:, 0:1344]
+    base = 320
+    ts_ = gath("s", T.FB[:, base:base + 512], FA, T.L0[:, 0:32], [code, la, ida])
+    tv = gath("v", T.FB[:, base + 512:base + 1024], FA, T.L0[:, 32:64], [code, lb, ida])
+
+    for k in range(3):
+        L, Ln = T["L%d" % k], T["L%d" % (k + 1)]
+        fb = [tv, ts_, idb, la, lb]
+        tv = gath("v", T.FA[:, base:base + XA], FB, L[:, 0:XA // 16], fb)
+        ts_ = gath("s", T.FA[:, base + XA:base + 1024], FB, L[:, XA // 16:64], fb)
+        fa = [tv, ts_]
+        t = relist(None, T.FA[:, base:base + XA], T.SC[:, 0:XA], XA, 0, 0, [tv])
+        la = ts(Ln[:, 0:XA // 16], T.SC[:, 15:XA:16], last16, add, op.add, op.add, [t])
+        gath("s", T.FB[:, base:base + XA], FA, Ln[:, 0:XA // 16], fa + [la])
+        t = relist(None, T.FA[:, base + XA:base + 1024], T.SC[:, XA:1024], 1024 - XA, 0, 0, [ts_])
+        lb = ts(Ln[:, XA // 16:64], T.SC[:, XA + 15:1024:16], last16, add, op.add, op.add, [t])
+        ts_ = gath("s", T.FB[:, base + XA:base + XB], FA, Ln[:, XA // 16:XB // 16], fa + [lb])
+        tv = gath("v", T.FB[:, base + XB:base + 1024], FA, Ln[:, XB // 16:64], fa + [lb])
+
+    fb = [tv, ts_, la, lb]
+    L = T.L3
+    tv = gath("v", T.t16[:, 768:896], FB, L[:, 48:56], fb)
+    ts_ = gath("s", T.t16[:, 896:1024], FB, L[:, 56:64], fb)
+    t = relist(None, T.t16[:, 768:1024], T.q16[:, 768:1024], 256, 0, 0, [tv, ts_])
+    lt = ts(T.LF[:, 48:64], T.q16[:, 783:1024:16], last16, add, op.add, op.add, [t])
+
+    straight, relays = routes(rank, T, topo)
+    loc = 0
+    for what in ("le", "list"):
+        if not straight and not relays:
+            break
+        need("gi", [le] if what == "le" else [lt])
+        src = mine[:, 0:64] if what == "le" else T.LF[:, 48:64]
+        if relays:
+            tr = []
+            for h, ranks, eng in relays:
+                rid, pid = topo.addr(h, core)
+                tr.append(RemoteDMATransfer(dst_ids=[DstId(rid=rid, pnc=pid)], dma_engine_mask=bits(eng),
+                                            remote_sem=T.sem.hle if what == "le" else T.sem.hli, srcs=[src],
+                                            dsts=[T.hle[:, :] if what == "le" else T.hli[:, :]]))
+                loc += len(eng)
+            g.remote_dma_fused(tr, local_sem=T.sem.loc)
+        if straight:
+            dst = mine[:, 0:64] if what == "le" else T["T%d" % rank][:, :]
+            loc += fan(g, T, topo, core, straight, src, dst, T.sem.le if what == "le" else T.sem["ar%d" % rank])
+
+    tv = gath("v", T.t16[:, 0:384], FB, L[:, 0:24], fb)
+    ts_ = gath("s", T.t16[:, 384:768], FB, L[:, 24:48], fb)
+    z0 = done("v", V.memset(T.V0[:, 64:320], 0.0))
+    t = relist(None, T.t16[:, 0:384], T.q16[:, 0:384], 384, 0, 0, [tv])
+    ts(T.LF[:, 0:24], T.q16[:, 15:384:16], last16, add, op.add, op.add, [t])
+    t = relist(None, T.t16[:, 384:768], T.q16[:, 384:768], 384, 0, 0, [ts_])
+    lr = ts(T.LF[:, 24:48], T.q16[:, 399:768:16], last16, add, op.add, op.add, [t])
+
+    prev = [z0]
+    total_le = 0
+    got = []
+    for k in range(rank):
+        hop = [c for c in routes(k, T, topo)[1] if rank in c[1]]
+        n = len(topo.engines(hop[0][0] if hop else T.cores[k], core))
+        total_le += n
+        got.append(("ar%d" % k, n))
+    for k in range(rank):
+        w, nx, lst = T["V%d" % k], T["V%d" % (k + 1)], T["T%d" % k]
+        deps = prev + [("le", total_le), got[k]]
+        a = gath("v", nx[:, 64:192], w[:, 0:320], lst[:, 0:8], deps)
+        b = gath("s", nx[:, 192:320], w[:, 0:320], lst[:, 8:16], deps)
+        prev = [a, b]
+
+    win = mine[:, 0:320]
+    deps = prev + [le, lt, lr]
+    for q, issue, a, b in (("v", "sy", 0, 320), ("s", "sy", 512, 832), ("v", "sy", 320, 512), ("s", "s", 832, 1024)):
+        t = gath(q, T.yb[:, a:b], win, T.LF[:, a // 16:b // 16], deps)
+        need(issue, [t])
+        done("dy", queue[issue].dma_start(out=T.y[:, a:b], in_=T.yb[:, a:b]), 16)
+    need("sy", [(s, cnt[s]) for s in ("dy", "v", "s", "pe", "gi", "dln", "dds", "dle")])
+    if loc:
+        g.wait_ge(T.sem.loc, loc)

@@ -5,6 +5,7 @@ OFF = 2047
 BIG = 1344
 XA = 352
 XB = 672
+SC1 = 864
 SCRATCH = {
     "xl": ("sbuf", [8, 64], "int32"), "xd": ("sbuf", [8, 64], "int32"), "lm": ("sbuf", [8, 64], "int32"),
     "lnf": ("sbuf", [8, 64], "float16"), "lastf": ("sbuf", [8, 64], "float16"), "dm": ("sbuf", [8, 64], "float16"),
@@ -21,6 +22,8 @@ SCRATCH = {
     "L0": ("sbuf", [128, 64], "uint16"), "L1": ("sbuf", [128, 64], "uint16"),
     "L2": ("sbuf", [128, 64], "uint16"), "L3": ("sbuf", [128, 64], "uint16"),
     "LF": ("sbuf", [128, 64], "uint16"),
+    "P": ("sbuf", [128, 320], "float32"), "p16": ("sbuf", [128, 256], "float16"), "pq": ("sbuf", [128, 256], "float16"),
+    "TP": ("sbuf", [128, 16], "uint16"), "VP": ("sbuf", [128, 384], "bfloat16"),
     "hle": ("sbuf", [128, 64], "bfloat16"), "hli": ("sbuf", [128, 16], "uint16"),
     "yb": ("sbuf", [128, 1024], "bfloat16"),
     "ps1": ("psum", [128, 512], "float32"), "ps2": ("psum", [128, 512], "float32"),
@@ -46,8 +49,8 @@ def routes(rank, T, topo):
     able.sort(key=lambda h: (topo.die(h) != topo.die(src), h))
     n = min(2, len(cross), len(able))
     eng = topo.engines(src, able[0])
-    w = len(eng) // n
-    return straight, [(able[i], cross[i::n], eng[i * w:(i + 1) * w]) for i in range(n)]
+    inner = [e for e in eng if e not in topo.engines(able[0], T.cores[cross[0]])]
+    return straight, [(able[i], cross[i::n], inner if i else eng) for i in range(n)]
 
 
 def fan(g, T, topo, core, ranks, src, dst, rsem):
@@ -55,9 +58,8 @@ def fan(g, T, topo, core, ranks, src, dst, rsem):
     for r in ranks:
         rid, pid = topo.addr(T.cores[r], core)
         ids.append(DstId(rid=rid, pnc=pid))
-    m = topo.mask(core, T.cores[ranks[0]])
-    g.remote_dma_fused([RemoteDMATransfer(dst_ids=ids, dma_engine_mask=m, remote_sem=rsem, srcs=[src],
-                                          dsts=[dst for _ in ranks])], local_sem=T.sem.loc)
+    g.remote_dma_fused([RemoteDMATransfer(dst_ids=ids, dma_engine_mask=topo.mask(core, T.cores[ranks[0]]), remote_sem=rsem,
+                                          srcs=[src], dsts=[dst for _ in ranks])], local_sem=T.sem.loc)
     return len(topo.engines(core, T.cores[ranks[0]]))
 
 
@@ -123,36 +125,40 @@ def rank_program(g, core, T, topo):
     ln = done("dln", SY.dma_start(out=T.xl[:, :], in_=T.ln[:, :]), 16)
     ds = done("dds", S.dma_start(out=T.xd[:, :], in_=T.ds[:, :]), 16)
     le = done("dle", SY.dma_start(out=mine[:, 0:64], in_=T.le[:, :]), 16)
+    flag = {"allow_small_or_imprecise_dtypes": True}
     ui = done("gi", g.iota(T.ui[:, :], [[1, 16]], 128, -1))
     ei = done("gi", g.iota(T.ei[:, :], [[1, 128]], 0, -16))
-    b0 = done("gi", g.iota(T.B[:, :], [[0, 1024]], 0, 0, allow_small_or_imprecise_dtypes=True))
-    ida = done("gi", g.iota(T.FA[:, 0:320], [[1, 320]], -OFF, 0, allow_small_or_imprecise_dtypes=True))
-    idb = done("gi", g.iota(T.FB[:, 0:320], [[1, 320]], -OFF, 0, allow_small_or_imprecise_dtypes=True))
+    ida = done("gi", g.iota(T.FA[:, 0:320], [[1, 320]], -OFF, 0, **flag))
+    idb = done("gi", g.iota(T.FB[:, 0:320], [[1, 320]], -OFF, 0, **flag))
+    idp = done("gi", g.iota(T.P[:, 0:64], [[1, 64]], -OFF, 0, **flag))
     a1 = done("v", V.memset(T.A[:, :], 1.0))
-    av63 = done("v", V.memset(T.av[:, 63:64], 1.0))
+    need("s", [a1])
+    b0 = done("s", S.activation(out=T.B[:, :], in_=T.A[:, 0:1024], func=fn.Copy, scale=0.0))
+    done("v", V.memset(T.av[:, 63:64], 1.0))
     uu = ts(T.uu[:, :], T.ui[:, :], 15, None, op.bitwise_and, None, [ui])
     es = ts(T.es[:, :], T.ei[:, :], 4, None, op.arith_shift_right, None, [ei])
     ma = ts(T.ma[:, :], T.uu[:, :], 0.0, -8192.0, op.is_equal, op.mult, [uu])
     mb = ts(T.mb[:, :], T.uu[:, :], 1.0, float(BIG), op.is_equal, op.mult, [uu])
     ee = ts(T.ee[:, :], T.es[:, :], 0.0, None, op.is_equal, None, [es])
     need("v", [ma, mb])
-    mt = done("v", V.tensor_tensor(out=T.mm[:, 0:16], in0=T.ma[:, :], in1=T.mb[:, :], op=op.add))
-    w = 16
-    m64 = mt
-    while w < XB:
-        n = min(w, XB - w)
-        need("s", [mt])
-        mt = done("s", S.activation(out=T.mm[:, w:w + n], in_=T.mm[:, 0:n], func=fn.Copy))
-        w += n
-        if w == 64:
-            m64 = mt
+    mtok = {16: done("v", V.tensor_tensor(out=T.mm[:, 0:16], in0=T.ma[:, :], in1=T.mb[:, :], op=op.add))}
+
+    def widen(to):
+        w = max(mtok)
+        while w < to:
+            n = min(w, to - w)
+            need("s", [mtok[w]])
+            mtok[w + n] = done("s", S.activation(out=T.mm[:, w:w + n], in_=T.mm[:, 0:n], func=fn.Copy))
+            w += n
+
     last16 = T.mb[:, 0:1]
 
-    def relist(out, src, tmp, n, c0, add, deps):
-        t = scan(tmp, T.mm[:, 0:n], src, 0.0, op.add, op.max, deps + [mt if n > 64 else m64, mb])
-        return t
+    def relist(src, tmp, n, deps):
+        return scan(tmp, T.mm[:, 0:n], src, 0.0, op.add, op.max, deps + [mtok[min(w for w in mtok if w >= n)], mb])
 
-    lnf = done("v", need("v", [ln]) or V.tensor_copy(out=T.lnf[:, :], in_=T.xl[:, :]))
+    widen(64)
+    need("v", [ln])
+    lnf = done("v", V.tensor_copy(out=T.lnf[:, :], in_=T.xl[:, :]))
     lm = ts(T.lm[:, :], T.xl[:, :], 0, None, op.is_gt, None, [ln])
     lastf = scan(T.lastf[:, :], T.A[0:8, 16:80], T.lnf[:, :], -1.0, op.add, op.add, [lnf, a1])
     need("pe", [lastf, ee])
@@ -161,31 +167,29 @@ def rank_program(g, core, T, topo):
     dm = done("v", V.tensor_tensor(out=T.dm[:, :], in0=T.xd[:, :], in1=T.lm[:, :], op=op.mult))
     need("pe", [dm])
     p2 = done("pe", PE.matmul(T.ps2[:, 0:64], T.ee[:, :], T.dm[:, :], True, True))
-    need("s", [p2, av63, a1])
-    done("s", S.activation(out=T.av[:, 0:63], in_=T.ps2[:, 1:64], func=fn.Identity, bias=1.0, scale=-1.0))
-    done("s", S.activation(out=T.bv[:, :], in_=T.ps2[:, 0:64], func=fn.Copy))
-    vals = done("s", S.activation(out=T.A[:, 15:16], in_=T.ps2[:, 0:1], func=fn.Identity, bias=1.0, scale=-1.0))
-    t = relist(None, T.ps1[:, 0:64], T.lsc[:, :], 64, 0, 0, [p1])
+    need("s", [p2])
+    avt = done("s", S.activation(out=T.av[:, 0:63], in_=T.ps2[:, 1:64], func=fn.Identity, bias=1.0, scale=-1.0))
+    bvt = done("s", S.activation(out=T.bv[:, :], in_=T.ps2[:, 0:64], func=fn.Copy))
+    first = done("s", S.activation(out=T.A[:, 15:16], in_=T.ps2[:, 0:1], func=fn.Identity, bias=1.0, scale=-1.0))
+    widen(512)
+    t = relist(T.ps1[:, 0:64], T.lsc[:, :], 64, [p1])
     lw = ts(T.lastw[:, :], T.lsc[:, 15:64:16], last16, -float(BIG), op.add, op.add, [t])
-    need("v", [lw, vals, b0])
-    done("v", V.tensor_copy(out=T.A[:, 16:1040].indirect(T.lastw[:, 0:4]), in_=T.av[:, :]))
-    sc2 = done("v", V.tensor_copy(out=T.B[:, 0:1024].indirect(T.lastw[:, 0:4]), in_=T.bv[:, :]))
-    h0 = scan(T.f16[:, 0:512], T.A[:, 15:527], T.B[:, 0:512], float(319 - OFF), op.add, op.add, [sc2])
-    need("s", [h0])
-    done("s", S.activation(out=T.FA[:, 320:832], in_=T.f16[:, 0:512], func=fn.Copy))
-    need("v", [h0])
-    hc = done("v", V.tensor_copy(out=T.lsc[:, 0:1], in_=T.f16[:, 511:512]))
-    h1 = scan(T.f16[:, 512:1024], T.A[:, 527:1039], T.B[:, 512:1024], T.lsc[:, 0:1], op.add, op.add, [hc])
-    need("s", [h1])
-    fcopy = done("s", S.activation(out=T.FA[:, 832:1344], in_=T.f16[:, 512:1024], func=fn.Copy))
-
+    need("v", [lw, avt])
+    sca = done("v", V.tensor_copy(out=T.A[:, 16:1040].indirect(T.lastw[:, 0:4]), in_=T.av[:, :]))
+    need("v", [bvt, b0])
+    scb = done("v", V.tensor_copy(out=T.B[:, 0:1024].indirect(T.lastw[:, 0:4]), in_=T.bv[:, :]))
+    h = scan(T.f16[:, :], T.A[:, 15:1039], T.B[:, :], float(319 - OFF), op.add, op.add, [sca, scb, first])
+    need("s", [h])
+    fcopy = done("s", S.activation(out=T.FA[:, 320:320 + SC1], in_=T.f16[:, 0:SC1], func=fn.Copy))
+    widen(XB)
+    need("v", [h])
+    vcopy = done("v", V.tensor_copy(out=T.FA[:, 320 + SC1:1344], in_=T.f16[:, SC1:1024]))
     add = float(OFF - BIG)
-    t = relist(None, T.f16[:, 0:512], T.r16[:, 0:512], 512, 0, 0, [h0])
-    la = ts(T.L0[:, 0:32], T.r16[:, 15:512:16], last16, add, op.add, op.add, [t])
-    t = relist(None, T.f16[:, 512:1024], T.r16[:, 512:1024], 512, 0, 0, [h1])
-    need("v", [fcopy, ida])
+    relist(T.f16[:, 0:512], T.r16[:, 0:512], 512, [h])
+    t = relist(T.f16[:, 512:1024], T.r16[:, 512:1024], 512, [h])
+    la = lb = ts(T.L0[:, :], T.r16[:, 15:1024:16], last16, add, op.add, op.add, [t])
+    need("v", [fcopy, vcopy, ida])
     code = done("v", V.tensor_copy(out=T.FA[:, 320:1344].indirect(T.lastw[:, 0:4]), in_=T.FA[:, 0:64]))
-    lb = ts(T.L0[:, 32:64], T.r16[:, 527:1024:16], last16, add, op.add, op.add, [t])
 
     FA, FB = T.FA[:, 0:1344], T.FB[:, 0:1344]
     base = 320
@@ -198,10 +202,10 @@ def rank_program(g, core, T, topo):
         tv = gath("v", T.FA[:, base:base + XA], FB, L[:, 0:XA // 16], fb)
         ts_ = gath("s", T.FA[:, base + XA:base + 1024], FB, L[:, XA // 16:64], fb)
         fa = [tv, ts_]
-        t = relist(None, T.FA[:, base:base + XA], T.SC[:, 0:XA], XA, 0, 0, [tv])
+        t = relist(T.FA[:, base:base + XA], T.SC[:, 0:XA], XA, [tv])
         la = ts(Ln[:, 0:XA // 16], T.SC[:, 15:XA:16], last16, add, op.add, op.add, [t])
         gath("s", T.FB[:, base:base + XA], FA, Ln[:, 0:XA // 16], fa + [la])
-        t = relist(None, T.FA[:, base + XA:base + 1024], T.SC[:, XA:1024], 1024 - XA, 0, 0, [ts_])
+        t = relist(T.FA[:, base + XA:base + 1024], T.SC[:, XA:1024], 1024 - XA, [ts_])
         lb = ts(Ln[:, XA // 16:64], T.SC[:, XA + 15:1024:16], last16, add, op.add, op.add, [t])
         ts_ = gath("s", T.FB[:, base + XA:base + XB], FA, Ln[:, XA // 16:XB // 16], fa + [lb])
         tv = gath("v", T.FB[:, base + XB:base + 1024], FA, Ln[:, XB // 16:64], fa + [lb])
@@ -210,7 +214,7 @@ def rank_program(g, core, T, topo):
     L = T.L3
     tv = gath("v", T.t16[:, 768:896], FB, L[:, 48:56], fb)
     ts_ = gath("s", T.t16[:, 896:1024], FB, L[:, 56:64], fb)
-    t = relist(None, T.t16[:, 768:1024], T.q16[:, 768:1024], 256, 0, 0, [tv, ts_])
+    t = relist(T.t16[:, 768:1024], T.q16[:, 768:1024], 256, [tv, ts_])
     lt = ts(T.LF[:, 48:64], T.q16[:, 783:1024:16], last16, add, op.add, op.add, [t])
 
     straight, relays = routes(rank, T, topo)
@@ -218,27 +222,35 @@ def rank_program(g, core, T, topo):
     for what in ("le", "list"):
         if not straight and not relays:
             break
-        need("gi", [le] if what == "le" else [lt])
-        src = mine[:, 0:64] if what == "le" else T.LF[:, 48:64]
+        early = what == "le"
+        need("gi", [le] if early else [lt])
+        src = mine[:, 0:64] if early else T.LF[:, 48:64]
+        calls = []
         if relays:
-            tr = []
-            for h, ranks, eng in relays:
-                rid, pid = topo.addr(h, core)
-                tr.append(RemoteDMATransfer(dst_ids=[DstId(rid=rid, pnc=pid)], dma_engine_mask=bits(eng),
-                                            remote_sem=T.sem.hle if what == "le" else T.sem.hli, srcs=[src],
-                                            dsts=[T.hle[:, :] if what == "le" else T.hli[:, :]]))
-                loc += len(eng)
-            g.remote_dma_fused(tr, local_sem=T.sem.loc)
+            calls.append((relays[0], None))
         if straight:
-            dst = mine[:, 0:64] if what == "le" else T["T%d" % rank][:, :]
-            loc += fan(g, T, topo, core, straight, src, dst, T.sem.le if what == "le" else T.sem["ar%d" % rank])
+            calls.append((None, straight if early else straight[:1]))
+        calls += [(x, None) for x in relays[1:]]
+        if straight[1:] and not early:
+            calls.append((None, straight[1:]))
+        for relay, ranks in calls:
+            if relay:
+                h, _, eng = relay
+                rid, pid = topo.addr(h, core)
+                g.remote_dma(out_ap=T.hle[:, :] if early else T.hli[:, :], in_ap=src,
+                             remote_sem=T.sem.hle if early else T.sem.hli, local_sem=T.sem.loc,
+                             pid=pid, routing_id=rid, dma_engine_mask=bits(eng))
+                loc += len(eng)
+            else:
+                dst = mine[:, 0:64] if early else T["T%d" % rank][:, :]
+                loc += fan(g, T, topo, core, ranks, src, dst, T.sem.le if early else T.sem["ar%d" % rank])
 
     tv = gath("v", T.t16[:, 0:384], FB, L[:, 0:24], fb)
     ts_ = gath("s", T.t16[:, 384:768], FB, L[:, 24:48], fb)
     z0 = done("v", V.memset(T.V0[:, 64:320], 0.0))
-    t = relist(None, T.t16[:, 0:384], T.q16[:, 0:384], 384, 0, 0, [tv])
+    t = relist(T.t16[:, 0:384], T.q16[:, 0:384], 384, [tv])
     ts(T.LF[:, 0:24], T.q16[:, 15:384:16], last16, add, op.add, op.add, [t])
-    t = relist(None, T.t16[:, 384:768], T.q16[:, 384:768], 384, 0, 0, [ts_])
+    t = relist(T.t16[:, 384:768], T.q16[:, 384:768], 384, [ts_])
     lr = ts(T.LF[:, 24:48], T.q16[:, 399:768:16], last16, add, op.add, op.add, [t])
 
     prev = [z0]
@@ -249,12 +261,36 @@ def rank_program(g, core, T, topo):
         n = len(topo.engines(hop[0][0] if hop else T.cores[k], core))
         total_le += n
         got.append(("ar%d" % k, n))
-    for k in range(rank):
-        w, nx, lst = T["V%d" % k], T["V%d" % (k + 1)], T["T%d" % k]
-        deps = prev + [("le", total_le), got[k]]
-        a = gath("v", nx[:, 64:192], w[:, 0:320], lst[:, 0:8], deps)
-        b = gath("s", nx[:, 192:320], w[:, 0:320], lst[:, 8:16], deps)
+    arrived = ("le", total_le)
+    far = [k for k in range(rank) if not topo.may_write(T.cores[k], core)]
+    pair = [k for k in range(1, rank - 1) if k - 1 in far and k not in far and k + 1 not in far][:1]
+    for k in pair:
+        t0, t1 = T["T%d" % k], T["T%d" % (k + 1)]
+        need("s", [arrived, got[k]])
+        a = done("s", S.activation(out=T.P[:, 192:320], in_=T.FA[:, 0:320].indirect(t0[:, 8:16]), func=fn.Identity, bias=64.0))
+        need("v", [got[k]])
+        b = done("v", V.tensor_scalar(out=T.P[:, 64:192], in0=T.FA[:, 0:320].indirect(t0[:, 0:8]), scalar1=64.0,
+                                      scalar2=None, op0=op.add))
+        done("s", S.activation(out=T.VP[:, 0:64], in_=T["V%d" % (k + 1)][:, 0:64], func=fn.Copy))
+        done("s", S.activation(out=T.VP[:, 64:128], in_=T["V%d" % k][:, 0:64], func=fn.Copy))
+        c = gath("v", T.p16[:, 0:128], T.P[:, :], t1[:, 0:8], [a, b, idp, got[k + 1]])
+        d = gath("s", T.p16[:, 128:256], T.P[:, :], t1[:, 8:16], [a, b, idp, got[k + 1]])
+        t = relist(T.p16[:, :], T.pq[:, :], 256, [c, d])
+        tp = ts(T.TP[:, :], T.pq[:, 15:256:16], last16, add, op.add, op.add, [t])
+        prev = prev + [d, tp]
+    k = 0
+    while k < rank:
+        if k in pair:
+            w, nx, lst = T.VP[:, 0:384], k + 2, T.TP
+            deps = prev
+        else:
+            w, nx, lst = T["V%d" % k][:, 0:320], k + 1, T["T%d" % k]
+            deps = prev + [arrived, got[k]]
+        out, c0 = (T.VP, 128) if nx in pair else (T["V%d" % nx], 64)
+        a = gath("v", out[:, c0:c0 + 128], w, lst[:, 0:8], deps)
+        b = gath("s", out[:, c0 + 128:c0 + 256], w, lst[:, 8:16], deps)
         prev = [a, b]
+        k = nx
 
     win = mine[:, 0:320]
     deps = prev + [le, lt, lr]

@@ -5,15 +5,17 @@ OFF = 2047
 BIG = 1344
 XA = 352
 XB = 672
-SC1 = 864
+XC = 320
+SC1 = 720
+HALF = 528
 SCRATCH = {
-    "xl": ("sbuf", [8, 64], "int32"), "xd": ("sbuf", [8, 64], "int32"), "lm": ("sbuf", [8, 64], "int32"),
-    "lnf": ("sbuf", [8, 64], "float16"), "lastf": ("sbuf", [8, 64], "float16"), "dm": ("sbuf", [8, 64], "float16"),
+    "xl": ("sbuf", [8, 64], "int32"), "xd": ("sbuf", [8, 64], "int32"),
+    "lastf": ("sbuf", [8, 64], "float16"), "df": ("sbuf", [8, 64], "float16"),
     "ei": ("sbuf", [8, 128], "int32"), "es": ("sbuf", [8, 128], "int32"), "ee": ("sbuf", [8, 128], "float16"),
     "ui": ("sbuf", [128, 16], "int32"), "uu": ("sbuf", [128, 16], "int32"),
     "ma": ("sbuf", [128, 16], "bfloat16"), "mb": ("sbuf", [128, 16], "bfloat16"), "mm": ("sbuf", [128, XB], "bfloat16"),
     "av": ("sbuf", [128, 64], "bfloat16"), "bv": ("sbuf", [128, 64], "bfloat16"),
-    "A": ("sbuf", [128, 1056], "bfloat16"), "B": ("sbuf", [128, 1024], "bfloat16"),
+    "A": ("sbuf", [128, 2 * HALF], "bfloat16"), "B": ("sbuf", [128, 1024], "bfloat16"),
     "lsc": ("sbuf", [128, 64], "float32"), "lastw": ("sbuf", [128, 4], "uint16"),
     "f16": ("sbuf", [128, 1024], "float16"), "r16": ("sbuf", [128, 1024], "float16"),
     "FA": ("sbuf", [128, 1344], "float32"), "FB": ("sbuf", [128, 1344], "float32"),
@@ -21,9 +23,8 @@ SCRATCH = {
     "t16": ("sbuf", [128, 1024], "float16"), "q16": ("sbuf", [128, 1024], "float16"),
     "L0": ("sbuf", [128, 64], "uint16"), "L1": ("sbuf", [128, 64], "uint16"),
     "L2": ("sbuf", [128, 64], "uint16"), "L3": ("sbuf", [128, 64], "uint16"),
+    "TA": ("sbuf", [128, 16], "uint16"), "TB": ("sbuf", [128, 16], "uint16"),
     "LF": ("sbuf", [128, 64], "uint16"),
-    "P": ("sbuf", [128, 320], "float32"), "p16": ("sbuf", [128, 256], "float16"), "pq": ("sbuf", [128, 256], "float16"),
-    "TP": ("sbuf", [128, 16], "uint16"), "VP": ("sbuf", [128, 384], "bfloat16"),
     "hle": ("sbuf", [128, 64], "bfloat16"), "hli": ("sbuf", [128, 16], "uint16"),
     "yb": ("sbuf", [128, 1024], "bfloat16"),
     "ps1": ("psum", [128, 512], "float32"), "ps2": ("psum", [128, 512], "float32"),
@@ -122,19 +123,19 @@ def rank_program(g, core, T, topo):
         return done("v", V.tensor_scalar(out=out, in0=in0, scalar1=s1, scalar2=s2, op0=op0, op1=op1))
 
     mine = T["V%d" % rank]
+    straight, relays = routes(rank, T, topo)
+    last = not straight and not relays
+    early_rank = rank < len(T.cores) // 2
     ln = done("dln", SY.dma_start(out=T.xl[:, :], in_=T.ln[:, :]), 16)
     ds = done("dds", S.dma_start(out=T.xd[:, :], in_=T.ds[:, :]), 16)
     le = done("dle", SY.dma_start(out=mine[:, 0:64], in_=T.le[:, :]), 16)
     flag = {"allow_small_or_imprecise_dtypes": True}
     ui = done("gi", g.iota(T.ui[:, :], [[1, 16]], 128, -1))
     ei = done("gi", g.iota(T.ei[:, :], [[1, 128]], 0, -16))
+    bg = done("gi", g.iota(T.B[:, 0:512], [[0, 512]], 0, 0, **flag))
     ida = done("gi", g.iota(T.FA[:, 0:320], [[1, 320]], -OFF, 0, **flag))
     idb = done("gi", g.iota(T.FB[:, 0:320], [[1, 320]], -OFF, 0, **flag))
-    idp = done("gi", g.iota(T.P[:, 0:64], [[1, 64]], -OFF, 0, **flag))
-    a1 = done("v", V.memset(T.A[:, :], 1.0))
-    need("s", [a1])
-    b0 = done("s", S.activation(out=T.B[:, :], in_=T.A[:, 0:1024], func=fn.Copy, scale=0.0))
-    done("v", V.memset(T.av[:, 63:64], 1.0))
+    a1 = done("v", V.memset(T.A[:, 0:HALF], 1.0))
     uu = ts(T.uu[:, :], T.ui[:, :], 15, None, op.bitwise_and, None, [ui])
     es = ts(T.es[:, :], T.ei[:, :], 4, None, op.arith_shift_right, None, [ei])
     ma = ts(T.ma[:, :], T.uu[:, :], 0.0, -8192.0, op.is_equal, op.mult, [uu])
@@ -142,6 +143,8 @@ def rank_program(g, core, T, topo):
     ee = ts(T.ee[:, :], T.es[:, :], 0.0, None, op.is_equal, None, [es])
     need("v", [ma, mb])
     mtok = {16: done("v", V.tensor_tensor(out=T.mm[:, 0:16], in0=T.ma[:, :], in1=T.mb[:, :], op=op.add))}
+    z0 = done("v", V.memset(T.V0[:, 64:320], 0.0))
+    av63 = done("v", V.memset(T.av[:, 63:64], 1.0))
 
     def widen(to):
         w = max(mtok)
@@ -151,44 +154,48 @@ def rank_program(g, core, T, topo):
             mtok[w + n] = done("s", S.activation(out=T.mm[:, w:w + n], in_=T.mm[:, 0:n], func=fn.Copy))
             w += n
 
+    need("s", [a1])
+    a2 = done("s", S.activation(out=T.A[:, HALF:2 * HALF], in_=T.A[:, 0:HALF], func=fn.Copy))
+    b0 = done("s", S.activation(out=T.B[:, 512:1024], in_=T.A[:, 16:HALF], func=fn.Copy, scale=0.0))
+    widen(128)
     last16 = T.mb[:, 0:1]
+    add = float(OFF - BIG)
 
     def relist(src, tmp, n, deps):
         return scan(tmp, T.mm[:, 0:n], src, 0.0, op.add, op.max, deps + [mtok[min(w for w in mtok if w >= n)], mb])
 
-    widen(64)
-    need("v", [ln])
-    lnf = done("v", V.tensor_copy(out=T.lnf[:, :], in_=T.xl[:, :]))
-    lm = ts(T.lm[:, :], T.xl[:, :], 0, None, op.is_gt, None, [ln])
-    lastf = scan(T.lastf[:, :], T.A[0:8, 16:80], T.lnf[:, :], -1.0, op.add, op.add, [lnf, a1])
+    def offs(out, picked, deps):
+        return ts(out, picked, last16, add, op.add, op.add, deps)
+
+    lastf = scan(T.lastf[:, :], T.A[0:8, 16:80], T.xl[:, :], -1.0, op.add, op.add, [ln, a1])
     need("pe", [lastf, ee])
     p1 = done("pe", PE.matmul(T.ps1[:, 0:64], T.ee[:, :], T.lastf[:, :], True, True))
-    need("v", [lm, ds])
-    dm = done("v", V.tensor_tensor(out=T.dm[:, :], in0=T.xd[:, :], in1=T.lm[:, :], op=op.mult))
-    need("pe", [dm])
-    p2 = done("pe", PE.matmul(T.ps2[:, 0:64], T.ee[:, :], T.dm[:, :], True, True))
+    need("v", [ds])
+    df = done("v", V.tensor_copy(out=T.df[:, :], in_=T.xd[:, :]))
+    need("pe", [df])
+    p2 = done("pe", PE.matmul(T.ps2[:, 0:64], T.ee[:, :], T.df[:, :], True, True))
     need("s", [p2])
     avt = done("s", S.activation(out=T.av[:, 0:63], in_=T.ps2[:, 1:64], func=fn.Identity, bias=1.0, scale=-1.0))
     bvt = done("s", S.activation(out=T.bv[:, :], in_=T.ps2[:, 0:64], func=fn.Copy))
+    need("s", [a2, b0])
     first = done("s", S.activation(out=T.A[:, 15:16], in_=T.ps2[:, 0:1], func=fn.Identity, bias=1.0, scale=-1.0))
     widen(512)
     t = relist(T.ps1[:, 0:64], T.lsc[:, :], 64, [p1])
     lw = ts(T.lastw[:, :], T.lsc[:, 15:64:16], last16, -float(BIG), op.add, op.add, [t])
-    need("v", [lw, avt])
+    need("v", [lw, avt, av63, a2])
     sca = done("v", V.tensor_copy(out=T.A[:, 16:1040].indirect(T.lastw[:, 0:4]), in_=T.av[:, :]))
-    need("v", [bvt, b0])
+    need("v", [bvt, b0, bg])
     scb = done("v", V.tensor_copy(out=T.B[:, 0:1024].indirect(T.lastw[:, 0:4]), in_=T.bv[:, :]))
     h = scan(T.f16[:, :], T.A[:, 15:1039], T.B[:, :], float(319 - OFF), op.add, op.add, [sca, scb, first])
     need("s", [h])
     fcopy = done("s", S.activation(out=T.FA[:, 320:320 + SC1], in_=T.f16[:, 0:SC1], func=fn.Copy))
     widen(XB)
-    need("v", [h])
-    vcopy = done("v", V.tensor_copy(out=T.FA[:, 320 + SC1:1344], in_=T.f16[:, SC1:1024]))
-    add = float(OFF - BIG)
+    need("gi", [h])
+    gcopy = done("gi", g.affine_select(T.FA[:, 320 + SC1:1344], T.f16[:, SC1:1024], [[0, 1024 - SC1]], op.is_equal, 0.0, 0, 0))
     relist(T.f16[:, 0:512], T.r16[:, 0:512], 512, [h])
     t = relist(T.f16[:, 512:1024], T.r16[:, 512:1024], 512, [h])
-    la = lb = ts(T.L0[:, :], T.r16[:, 15:1024:16], last16, add, op.add, op.add, [t])
-    need("v", [fcopy, vcopy, ida])
+    la = lb = offs(T.L0[:, :], T.r16[:, 15:1024:16], [t])
+    need("v", [fcopy, gcopy, ida])
     code = done("v", V.tensor_copy(out=T.FA[:, 320:1344].indirect(T.lastw[:, 0:4]), in_=T.FA[:, 0:64]))
 
     FA, FB = T.FA[:, 0:1344], T.FB[:, 0:1344]
@@ -196,32 +203,39 @@ def rank_program(g, core, T, topo):
     ts_ = gath("s", T.FB[:, base:base + 512], FA, T.L0[:, 0:32], [code, la, ida])
     tv = gath("v", T.FB[:, base + 512:base + 1024], FA, T.L0[:, 32:64], [code, lb, ida])
 
+    def tail(win, lst, c0, out, deps):
+        a = gath("v", T.t16[:, 768:896], win, lst[:, c0:c0 + 8], deps)
+        b = gath("s", T.t16[:, 896:1024], win, lst[:, c0 + 8:c0 + 16], deps)
+        t = relist(T.t16[:, 768:1024], T.q16[:, 768:1024], 256, [a, b])
+        return offs(out, T.q16[:, 783:1024:16], [t])
+
+    lt = None
     for k in range(3):
         L, Ln = T["L%d" % k], T["L%d" % (k + 1)]
+        ahead = k == 2 and early_rank
+        xa = XC if ahead else XA
         fb = [tv, ts_, idb, la, lb]
-        tv = gath("v", T.FA[:, base:base + XA], FB, L[:, 0:XA // 16], fb)
-        ts_ = gath("s", T.FA[:, base + XA:base + 1024], FB, L[:, XA // 16:64], fb)
+        tv = gath("v", T.FA[:, base:base + xa], FB, L[:, 0:xa // 16], fb)
+        ts_ = gath("s", T.FA[:, base + xa:base + 1024], FB, L[:, xa // 16:64], fb)
         fa = [tv, ts_]
-        t = relist(T.FA[:, base:base + XA], T.SC[:, 0:XA], XA, [tv])
-        la = ts(Ln[:, 0:XA // 16], T.SC[:, 15:XA:16], last16, add, op.add, op.add, [t])
+        if ahead:
+            t = relist(T.FB[:, base + 768:base + 1024], T.SC[:, 768:1024], 256, fb)
+            lt = offs(T.TA[:, :], T.SC[:, 783:1024:16], [t])
+            lt = tail(FA, T.TA, 0, T.TB[:, :], fa + [lt])
+            lt = tail(FA, T.TB, 0, T.LF[:, 48:64], fa + [lt])
+        t = relist(T.FA[:, base:base + XA], T.SC[:, 0:XA], XA, fa if ahead else [tv])
+        la = offs(Ln[:, 0:XA // 16], T.SC[:, 15:XA:16], [t])
         gath("s", T.FB[:, base:base + XA], FA, Ln[:, 0:XA // 16], fa + [la])
-        t = relist(T.FA[:, base + XA:base + 1024], T.SC[:, XA:1024], 1024 - XA, [ts_])
-        lb = ts(Ln[:, XA // 16:64], T.SC[:, XA + 15:1024:16], last16, add, op.add, op.add, [t])
+        t = relist(T.FA[:, base + XA:base + 1024], T.SC[:, XA:1024], 1024 - XA, fa)
+        lb = offs(Ln[:, XA // 16:64], T.SC[:, XA + 15:1024:16], [t])
         ts_ = gath("s", T.FB[:, base + XA:base + XB], FA, Ln[:, XA // 16:XB // 16], fa + [lb])
         tv = gath("v", T.FB[:, base + XB:base + 1024], FA, Ln[:, XB // 16:64], fa + [lb])
-
     fb = [tv, ts_, la, lb]
-    L = T.L3
-    tv = gath("v", T.t16[:, 768:896], FB, L[:, 48:56], fb)
-    ts_ = gath("s", T.t16[:, 896:1024], FB, L[:, 56:64], fb)
-    t = relist(T.t16[:, 768:1024], T.q16[:, 768:1024], 256, [tv, ts_])
-    lt = ts(T.LF[:, 48:64], T.q16[:, 783:1024:16], last16, add, op.add, op.add, [t])
+    if not early_rank and not last:
+        lt = tail(FB, T.L3, 48, T.LF[:, 48:64], fb)
 
-    straight, relays = routes(rank, T, topo)
     loc = 0
-    for what in ("le", "list"):
-        if not straight and not relays:
-            break
+    for what in () if last else ("le", "list"):
         early = what == "le"
         need("gi", [le] if early else [lt])
         src = mine[:, 0:64] if early else T.LF[:, 48:64]
@@ -245,13 +259,13 @@ def rank_program(g, core, T, topo):
                 dst = mine[:, 0:64] if early else T["T%d" % rank][:, :]
                 loc += fan(g, T, topo, core, ranks, src, dst, T.sem.le if early else T.sem["ar%d" % rank])
 
-    tv = gath("v", T.t16[:, 0:384], FB, L[:, 0:24], fb)
-    ts_ = gath("s", T.t16[:, 384:768], FB, L[:, 24:48], fb)
-    z0 = done("v", V.memset(T.V0[:, 64:320], 0.0))
-    t = relist(T.t16[:, 0:384], T.q16[:, 0:384], 384, [tv])
-    ts(T.LF[:, 0:24], T.q16[:, 15:384:16], last16, add, op.add, op.add, [t])
-    t = relist(T.t16[:, 384:768], T.q16[:, 384:768], 384, [ts_])
-    lr = ts(T.LF[:, 24:48], T.q16[:, 399:768:16], last16, add, op.add, op.add, [t])
+    n = 1024 if last else 768
+    m = n // 2
+    tv = gath("v", T.t16[:, 0:m], FB, T.L3[:, 0:m // 16], fb)
+    ts_ = gath("s", T.t16[:, m:n], FB, T.L3[:, m // 16:n // 16], fb)
+    relist(T.t16[:, 0:m], T.q16[:, 0:m], m, [tv])
+    t = relist(T.t16[:, m:n], T.q16[:, m:n], m, [ts_])
+    lr = offs(T.LF[:, 0:n // 16], T.q16[:, 15:n:16], [t])
 
     prev = [z0]
     total_le = 0
@@ -261,39 +275,15 @@ def rank_program(g, core, T, topo):
         n = len(topo.engines(hop[0][0] if hop else T.cores[k], core))
         total_le += n
         got.append(("ar%d" % k, n))
-    arrived = ("le", total_le)
-    far = [k for k in range(rank) if not topo.may_write(T.cores[k], core)]
-    pair = [k for k in range(1, rank - 1) if k - 1 in far and k not in far and k + 1 not in far][:1]
-    for k in pair:
-        t0, t1 = T["T%d" % k], T["T%d" % (k + 1)]
-        need("s", [arrived, got[k]])
-        a = done("s", S.activation(out=T.P[:, 192:320], in_=T.FA[:, 0:320].indirect(t0[:, 8:16]), func=fn.Identity, bias=64.0))
-        need("v", [got[k]])
-        b = done("v", V.tensor_scalar(out=T.P[:, 64:192], in0=T.FA[:, 0:320].indirect(t0[:, 0:8]), scalar1=64.0,
-                                      scalar2=None, op0=op.add))
-        done("s", S.activation(out=T.VP[:, 0:64], in_=T["V%d" % (k + 1)][:, 0:64], func=fn.Copy))
-        done("s", S.activation(out=T.VP[:, 64:128], in_=T["V%d" % k][:, 0:64], func=fn.Copy))
-        c = gath("v", T.p16[:, 0:128], T.P[:, :], t1[:, 0:8], [a, b, idp, got[k + 1]])
-        d = gath("s", T.p16[:, 128:256], T.P[:, :], t1[:, 8:16], [a, b, idp, got[k + 1]])
-        t = relist(T.p16[:, :], T.pq[:, :], 256, [c, d])
-        tp = ts(T.TP[:, :], T.pq[:, 15:256:16], last16, add, op.add, op.add, [t])
-        prev = prev + [d, tp]
-    k = 0
-    while k < rank:
-        if k in pair:
-            w, nx, lst = T.VP[:, 0:384], k + 2, T.TP
-            deps = prev
-        else:
-            w, nx, lst = T["V%d" % k][:, 0:320], k + 1, T["T%d" % k]
-            deps = prev + [arrived, got[k]]
-        out, c0 = (T.VP, 128) if nx in pair else (T["V%d" % nx], 64)
-        a = gath("v", out[:, c0:c0 + 128], w, lst[:, 0:8], deps)
-        b = gath("s", out[:, c0 + 128:c0 + 256], w, lst[:, 8:16], deps)
+    for k in range(rank):
+        w, nx, lst = T["V%d" % k], T["V%d" % (k + 1)], T["T%d" % k]
+        deps = prev + [("le", total_le), got[k]]
+        a = gath("v", nx[:, 64:192], w[:, 0:320], lst[:, 0:8], deps)
+        b = gath("s", nx[:, 192:320], w[:, 0:320], lst[:, 8:16], deps)
         prev = [a, b]
-        k = nx
 
     win = mine[:, 0:320]
-    deps = prev + [le, lt, lr]
+    deps = prev + [le, lr] + ([] if last else [lt])
     for q, issue, a, b in (("v", "sy", 0, 320), ("s", "sy", 512, 832), ("v", "sy", 320, 512), ("s", "s", 832, 1024)):
         t = gath(q, T.yb[:, a:b], win, T.LF[:, a // 16:b // 16], deps)
         need(issue, [t])

@@ -3,32 +3,39 @@ from concourse.mybir import AluOpType, ActivationFunctionType
 
 OFF = 2047
 BIG = 1344
-XA = 352
-XB = 672
-XC = 320
+POW = [1, 2, 3, 6, 9, 18, 27, 54]
+EARLY = 2
+H = 512
+XV = 352
+B1 = 704
+XY = 416
+XZ = 768
+XC = 352
 SC1 = 720
+BG = 736
 HALF = 528
 SCRATCH = {
     "xl": ("sbuf", [8, 64], "int32"), "xd": ("sbuf", [8, 64], "int32"),
     "lastf": ("sbuf", [8, 64], "float16"), "df": ("sbuf", [8, 64], "float16"),
-    "ei": ("sbuf", [8, 128], "int32"), "es": ("sbuf", [8, 128], "int32"), "ee": ("sbuf", [8, 128], "float16"),
+    "ei": ("sbuf", [8, 128], "int32"), "ee": ("sbuf", [8, 128], "float16"),
     "ui": ("sbuf", [128, 16], "int32"), "uu": ("sbuf", [128, 16], "int32"),
-    "ma": ("sbuf", [128, 16], "bfloat16"), "mb": ("sbuf", [128, 16], "bfloat16"), "mm": ("sbuf", [128, XB], "bfloat16"),
-    "av": ("sbuf", [128, 64], "bfloat16"), "bv": ("sbuf", [128, 64], "bfloat16"),
+    "ma": ("sbuf", [128, 16], "bfloat16"), "mb": ("sbuf", [128, 16], "bfloat16"), "mm": ("sbuf", [128, 512], "bfloat16"),
+    "av": ("sbuf", [128, 64], "bfloat16"), "bv": ("sbuf", [128, 64], "bfloat16"), "ob": ("sbuf", [128, 1], "float32"),
     "A": ("sbuf", [128, 2 * HALF], "bfloat16"), "B": ("sbuf", [128, 1024], "bfloat16"),
     "lsc": ("sbuf", [128, 64], "float32"), "lastw": ("sbuf", [128, 4], "uint16"),
     "f16": ("sbuf", [128, 1024], "float16"), "r16": ("sbuf", [128, 1024], "float16"),
-    "FA": ("sbuf", [128, 1344], "float32"), "FB": ("sbuf", [128, 1344], "float32"),
     "SC": ("sbuf", [128, 1024], "float32"),
     "t16": ("sbuf", [128, 1024], "float16"), "q16": ("sbuf", [128, 1024], "float16"),
-    "L0": ("sbuf", [128, 64], "uint16"), "L1": ("sbuf", [128, 64], "uint16"),
-    "L2": ("sbuf", [128, 64], "uint16"), "L3": ("sbuf", [128, 64], "uint16"),
+    "L1": ("sbuf", [128, 64], "uint16"), "L3": ("sbuf", [128, 64], "uint16"),
+    "L9": ("sbuf", [128, 64], "uint16"), "L27": ("sbuf", [128, 64], "uint16"),
     "TA": ("sbuf", [128, 16], "uint16"), "TB": ("sbuf", [128, 16], "uint16"),
     "LF": ("sbuf", [128, 64], "uint16"),
     "hle": ("sbuf", [128, 64], "bfloat16"), "hli": ("sbuf", [128, 16], "uint16"),
     "yb": ("sbuf", [128, 1024], "bfloat16"),
     "ps1": ("psum", [128, 512], "float32"), "ps2": ("psum", [128, 512], "float32"),
 }
+for _k in range(4):
+    SCRATCH["W%d" % _k] = ("sbuf", [128, 1344], "float32")
 for _k in range(8):
     SCRATCH["V%d" % _k] = ("sbuf", [128, 320], "bfloat16")
     SCRATCH["T%d" % _k] = ("sbuf", [128, 16], "uint16")
@@ -125,26 +132,29 @@ def rank_program(g, core, T, topo):
     mine = T["V%d" % rank]
     straight, relays = routes(rank, T, topo)
     last = not straight and not relays
-    early_rank = rank < len(T.cores) // 2
+    early_rank = rank < EARLY
     ln = done("dln", SY.dma_start(out=T.xl[:, :], in_=T.ln[:, :]), 16)
     ds = done("dds", S.dma_start(out=T.xd[:, :], in_=T.ds[:, :]), 16)
     le = done("dle", SY.dma_start(out=mine[:, 0:64], in_=T.le[:, :]), 16)
     flag = {"allow_small_or_imprecise_dtypes": True}
+    add = float(OFF - BIG)
+    ident = {}
+
+    def roots(i):
+        ident[i] = done("gi", g.iota(T["W%d" % i][:, 0:320], [[1, 320]], -OFF, 0, **flag))
+
     ui = done("gi", g.iota(T.ui[:, :], [[1, 16]], 128, -1))
-    ei = done("gi", g.iota(T.ei[:, :], [[1, 128]], 0, -16))
-    bg = done("gi", g.iota(T.B[:, 0:512], [[0, 512]], 0, 0, **flag))
-    ida = done("gi", g.iota(T.FA[:, 0:320], [[1, 320]], -OFF, 0, **flag))
-    idb = done("gi", g.iota(T.FB[:, 0:320], [[1, 320]], -OFF, 0, **flag))
+    ei = done("gi", g.iota(T.ei[:, :], [[1, 8], [0, 16]], 0, -1))
+    bh = done("gi", g.iota(T.B[:, 0:1024 - BG], [[0, 1024 - BG]], 0, 0, **flag))
+    bg = done("gi", g.iota(T.B[:, 1024 - BG:BG], [[0, 2 * BG - 1024]], 0, 0, **flag))
+    roots(0)
     a1 = done("v", V.memset(T.A[:, 0:HALF], 1.0))
     uu = ts(T.uu[:, :], T.ui[:, :], 15, None, op.bitwise_and, None, [ui])
-    es = ts(T.es[:, :], T.ei[:, :], 4, None, op.arith_shift_right, None, [ei])
     ma = ts(T.ma[:, :], T.uu[:, :], 0.0, -8192.0, op.is_equal, op.mult, [uu])
     mb = ts(T.mb[:, :], T.uu[:, :], 1.0, float(BIG), op.is_equal, op.mult, [uu])
-    ee = ts(T.ee[:, :], T.es[:, :], 0.0, None, op.is_equal, None, [es])
+    ee = ts(T.ee[:, :], T.ei[:, :], 0.0, None, op.is_equal, None, [ei])
     need("v", [ma, mb])
     mtok = {16: done("v", V.tensor_tensor(out=T.mm[:, 0:16], in0=T.ma[:, :], in1=T.mb[:, :], op=op.add))}
-    z0 = done("v", V.memset(T.V0[:, 64:320], 0.0))
-    av63 = done("v", V.memset(T.av[:, 63:64], 1.0))
 
     def widen(to):
         w = max(mtok)
@@ -156,10 +166,8 @@ def rank_program(g, core, T, topo):
 
     need("s", [a1])
     a2 = done("s", S.activation(out=T.A[:, HALF:2 * HALF], in_=T.A[:, 0:HALF], func=fn.Copy))
-    b0 = done("s", S.activation(out=T.B[:, 512:1024], in_=T.A[:, 16:HALF], func=fn.Copy, scale=0.0))
-    widen(128)
+    widen(64)
     last16 = T.mb[:, 0:1]
-    add = float(OFF - BIG)
 
     def relist(src, tmp, n, deps):
         return scan(tmp, T.mm[:, 0:n], src, 0.0, op.add, op.max, deps + [mtok[min(w for w in mtok if w >= n)], mb])
@@ -172,13 +180,17 @@ def rank_program(g, core, T, topo):
     p1 = done("pe", PE.matmul(T.ps1[:, 0:64], T.ee[:, :], T.lastf[:, :], True, True))
     need("v", [ds])
     df = done("v", V.tensor_copy(out=T.df[:, :], in_=T.xd[:, :]))
+    av63 = done("v", V.memset(T.av[:, 63:64], 1.0))
+    ob = ts(T.ob[:, :], T.mb[:, 0:1], add, None, op.add, None, [mb])
     need("pe", [df])
     p2 = done("pe", PE.matmul(T.ps2[:, 0:64], T.ee[:, :], T.df[:, :], True, True))
     need("s", [p2])
     avt = done("s", S.activation(out=T.av[:, 0:63], in_=T.ps2[:, 1:64], func=fn.Identity, bias=1.0, scale=-1.0))
     bvt = done("s", S.activation(out=T.bv[:, :], in_=T.ps2[:, 0:64], func=fn.Copy))
-    need("s", [a2, b0])
+    need("s", [a2])
     first = done("s", S.activation(out=T.A[:, 15:16], in_=T.ps2[:, 0:1], func=fn.Identity, bias=1.0, scale=-1.0))
+    need("s", [bh])
+    b0 = done("s", S.activation(out=T.B[:, BG:1024], in_=T.B[:, 0:1024 - BG], func=fn.Copy))
     widen(512)
     t = relist(T.ps1[:, 0:64], T.lsc[:, :], 64, [p1])
     lw = ts(T.lastw[:, :], T.lsc[:, 15:64:16], last16, -float(BIG), op.add, op.add, [t])
@@ -188,51 +200,88 @@ def rank_program(g, core, T, topo):
     scb = done("v", V.tensor_copy(out=T.B[:, 0:1024].indirect(T.lastw[:, 0:4]), in_=T.bv[:, :]))
     h = scan(T.f16[:, :], T.A[:, 15:1039], T.B[:, :], float(319 - OFF), op.add, op.add, [sca, scb, first])
     need("s", [h])
-    fcopy = done("s", S.activation(out=T.FA[:, 320:320 + SC1], in_=T.f16[:, 0:SC1], func=fn.Copy))
-    widen(XB)
+    fcopy = done("s", S.activation(out=T.W0[:, 320:320 + SC1], in_=T.f16[:, 0:SC1], func=fn.Copy))
     need("gi", [h])
-    gcopy = done("gi", g.affine_select(T.FA[:, 320 + SC1:1344], T.f16[:, SC1:1024], [[0, 1024 - SC1]], op.is_equal, 0.0, 0, 0))
+    gcopy = done("gi", g.affine_select(T.W0[:, 320 + SC1:1344], T.f16[:, SC1:1024], [[0, 1024 - SC1]], op.is_equal, 0.0, 0, 0))
+    for i in (1, 2, 3):
+        roots(i)
+    z0 = done("gi", g.iota(T.V0[:, 64:320], [[0, 256]], 0, 0, **flag))
     relist(T.f16[:, 0:512], T.r16[:, 0:512], 512, [h])
     t = relist(T.f16[:, 512:1024], T.r16[:, 512:1024], 512, [h])
-    la = lb = offs(T.L0[:, :], T.r16[:, 15:1024:16], [t])
-    need("v", [fcopy, gcopy, ida])
-    code = done("v", V.tensor_copy(out=T.FA[:, 320:1344].indirect(T.lastw[:, 0:4]), in_=T.FA[:, 0:64]))
+    l1 = offs(T.L1[:, :], T.r16[:, 15:1024:16], [t])
+    need("v", [fcopy, gcopy, ident[0]])
+    code = done("v", V.tensor_copy(out=T.W0[:, 320:1344].indirect(T.lastw[:, 0:4]), in_=T.W0[:, 0:64]))
 
-    FA, FB = T.FA[:, 0:1344], T.FB[:, 0:1344]
     base = 320
-    ts_ = gath("s", T.FB[:, base:base + 512], FA, T.L0[:, 0:32], [code, la, ida])
-    tv = gath("v", T.FB[:, base + 512:base + 1024], FA, T.L0[:, 32:64], [code, lb, ida])
+    LIST = {1: T.L1, 3: T.L3, 9: T.L9, 27: T.L27}
+    WIN = {k: T["W%d" % (i % 4)] for i, k in enumerate(POW)}
+    made = {1: [(0, 1024, code)]}
+    listed = {1: [(0, 1024, l1)]}
+    readers = {}
 
-    def tail(win, lst, c0, out, deps):
+    def after(where, a, b):
+        return [x[2] for x in where if x[0] < b and a < x[1]]
+
+    def whole(k):
+        return [ident[POW.index(k) % 4]] + after(made[k], 0, 1024)
+
+    def jump(q, a_, b_, c0, c1):
+        k = a_ + b_
+        i = POW.index(k)
+        old = readers.get(POW[i - 4], []) if i >= 4 else []
+        deps = [ident[POW.index(a_) % 4]] + after(made[a_], 0, c1) + after(listed[b_], c0, c1) + old
+        t = gath(q, WIN[k][:, base + c0:base + c1], WIN[a_][:, 0:base + c1], LIST[b_][:, c0 // 16:c1 // 16], deps)
+        readers.setdefault(a_, []).append(t)
+        made.setdefault(k, []).append((c0, c1, t))
+
+    def pick(k, c0, c1):
+        return relist(WIN[k][:, base + c0:base + c1], T.SC[:, c0:c1], c1 - c0, after(made[k], c0, c1))
+
+    def lists(q, k, c0, c1, toks):
+        out, src = LIST[k][:, c0 // 16:c1 // 16], T.SC[:, c0 + 15:c1:16]
+        if q == "v":
+            t = offs(out, src, toks)
+        else:
+            need("s", toks + [ob])
+            t = done("s", S.activation(out=out, in_=src, func=fn.Identity, bias=T.ob[:, 0:1]))
+        listed.setdefault(k, []).append((c0, c1, t))
+
+    def tail(k, lst, c0, out, deps):
+        deps = deps + whole(k)
+        win = WIN[k][:, :]
         a = gath("v", T.t16[:, 768:896], win, lst[:, c0:c0 + 8], deps)
         b = gath("s", T.t16[:, 896:1024], win, lst[:, c0 + 8:c0 + 16], deps)
         t = relist(T.t16[:, 768:1024], T.q16[:, 768:1024], 256, [a, b])
         return offs(out, T.q16[:, 783:1024:16], [t])
 
+    jump("s", 1, 1, 0, 256)
+    jump("v", 1, 1, 256, 512)
+    jump("s", 1, 1, 512, 768)
+    jump("v", 1, 1, 768, 1024)
     lt = None
-    for k in range(3):
-        L, Ln = T["L%d" % k], T["L%d" % (k + 1)]
-        ahead = k == 2 and early_rank
-        xa = XC if ahead else XA
-        fb = [tv, ts_, idb, la, lb]
-        tv = gath("v", T.FA[:, base:base + xa], FB, L[:, 0:xa // 16], fb)
-        ts_ = gath("s", T.FA[:, base + xa:base + 1024], FB, L[:, xa // 16:64], fb)
-        fa = [tv, ts_]
-        if ahead:
-            t = relist(T.FB[:, base + 768:base + 1024], T.SC[:, 768:1024], 256, fb)
+    for k in (1, 3, 9):
+        if k == 9 and early_rank:
+            jump("s", 18, 9, XC, 1024)
+            jump("v", 18, 9, 0, XC)
+            t = relist(WIN[18][:, base + 768:base + 1024], T.SC[:, 768:1024], 256, after(made[18], 768, 1024))
             lt = offs(T.TA[:, :], T.SC[:, 783:1024:16], [t])
-            lt = tail(FA, T.TA, 0, T.TB[:, :], fa + [lt])
-            lt = tail(FA, T.TB, 0, T.LF[:, 48:64], fa + [lt])
-        t = relist(T.FA[:, base:base + XA], T.SC[:, 0:XA], XA, fa if ahead else [tv])
-        la = offs(Ln[:, 0:XA // 16], T.SC[:, 15:XA:16], [t])
-        gath("s", T.FB[:, base:base + XA], FA, Ln[:, 0:XA // 16], fa + [la])
-        t = relist(T.FA[:, base + XA:base + 1024], T.SC[:, XA:1024], 1024 - XA, fa)
-        lb = offs(Ln[:, XA // 16:64], T.SC[:, XA + 15:1024:16], [t])
-        ts_ = gath("s", T.FB[:, base + XA:base + XB], FA, Ln[:, XA // 16:XB // 16], fa + [lb])
-        tv = gath("v", T.FB[:, base + XB:base + 1024], FA, Ln[:, XB // 16:64], fa + [lb])
-    fb = [tv, ts_, la, lb]
+            lt = tail(27, T.TA, 0, T.TB[:, :], [lt])
+            lt = tail(27, T.TB, 0, T.LF[:, 48:64], [lt])
+        else:
+            jump("s", 2 * k, k, XV, H)
+            jump("v", 2 * k, k, 0, XV)
+            jump("s", 2 * k, k, H, B1)
+            jump("s", 2 * k, k, B1, 1024)
+        lists("s", 3 * k, 0, H, [pick(3 * k, 0, H)])
+        jump("s", 3 * k, 3 * k, 0, XY)
+        t = [pick(3 * k, H, B1), pick(3 * k, B1, 1024)]
+        jump("v", 3 * k, 3 * k, XY, H)
+        lists("v", 3 * k, H, 1024, t)
+        jump("v", 3 * k, 3 * k, H, XZ)
+        jump("s", 3 * k, 3 * k, XZ, 1024)
+    fb = whole(54) + after(listed[27], 0, 1024)
     if not early_rank and not last:
-        lt = tail(FB, T.L3, 48, T.LF[:, 48:64], fb)
+        lt = tail(54, T.L27, 48, T.LF[:, 48:64], fb)
 
     loc = 0
     for what in () if last else ("le", "list"):
@@ -261,8 +310,9 @@ def rank_program(g, core, T, topo):
 
     n = 1024 if last else 768
     m = n // 2
-    tv = gath("v", T.t16[:, 0:m], FB, T.L3[:, 0:m // 16], fb)
-    ts_ = gath("s", T.t16[:, m:n], FB, T.L3[:, m // 16:n // 16], fb)
+    FB = WIN[54][:, :]
+    tv = gath("v", T.t16[:, 0:m], FB, T.L27[:, 0:m // 16], fb)
+    ts_ = gath("s", T.t16[:, m:n], FB, T.L27[:, m // 16:n // 16], fb)
     relist(T.t16[:, 0:m], T.q16[:, 0:m], m, [tv])
     t = relist(T.t16[:, m:n], T.q16[:, m:n], m, [ts_])
     lr = offs(T.LF[:, 0:n // 16], T.q16[:, 15:n:16], [t])

from concourse.bass import DstId, RemoteDMATransfer
from concourse.mybir import AluOpType, ActivationFunctionType

OFF = 2047
BIG = 1344
POW = [1, 2, 3, 6, 9, 18, 27, 54]
EARLY = 2
H = 512
XV = 352
B1 = 704
XY = 416
XZ = 768
XC = 352
SC1 = 720
BG = 736
HALF = 528
SCRATCH = {
    "xl": ("sbuf", [8, 64], "int32"), "xd": ("sbuf", [8, 64], "int32"),
    "lastf": ("sbuf", [8, 64], "float16"), "df": ("sbuf", [8, 64], "float16"),
    "ei": ("sbuf", [8, 128], "int32"), "ee": ("sbuf", [8, 128], "float16"),
    "ui": ("sbuf", [128, 16], "int32"), "uu": ("sbuf", [128, 16], "int32"),
    "ma": ("sbuf", [128, 16], "bfloat16"), "mb": ("sbuf", [128, 16], "bfloat16"), "mm": ("sbuf", [128, 512], "bfloat16"),
    "av": ("sbuf", [128, 64], "bfloat16"), "bv": ("sbuf", [128, 64], "bfloat16"), "ob": ("sbuf", [128, 1], "float32"),
    "A": ("sbuf", [128, 2 * HALF], "bfloat16"), "B": ("sbuf", [128, 1024], "bfloat16"),
    "lsc": ("sbuf", [128, 64], "float32"), "lastw": ("sbuf", [128, 4], "uint16"),
    "f16": ("sbuf", [128, 1024], "float16"), "r16": ("sbuf", [128, 1024], "float16"),
    "SC": ("sbuf", [128, 1024], "float32"),
    "t16": ("sbuf", [128, 1024], "float16"), "q16": ("sbuf", [128, 1024], "float16"),
    "L1": ("sbuf", [128, 64], "uint16"), "L3": ("sbuf", [128, 64], "uint16"),
    "L9": ("sbuf", [128, 64], "uint16"), "L27": ("sbuf", [128, 64], "uint16"),
    "TA": ("sbuf", [128, 16], "uint16"), "TB": ("sbuf", [128, 16], "uint16"),
    "LF": ("sbuf", [128, 64], "uint16"),
    "hle": ("sbuf", [128, 64], "bfloat16"), "hli": ("sbuf", [128, 16], "uint16"),
    "yb": ("sbuf", [128, 1024], "bfloat16"),
    "ps1": ("psum", [128, 512], "float32"), "ps2": ("psum", [128, 512], "float32"),
}
for _k in range(4):
    SCRATCH["W%d" % _k] = ("sbuf", [128, 1344], "float32")
for _k in range(8):
    SCRATCH["V%d" % _k] = ("sbuf", [128, 320], "bfloat16")
    SCRATCH["T%d" % _k] = ("sbuf", [128, 16], "uint16")
SEMAPHORES = ["v", "s", "pe", "gi", "dln", "dds", "dle", "dy", "loc", "le", "hle", "hli"] + ["ar%d" % k for k in range(8)]


def bits(engines):
    return sum(1 << e for e in engines)


def routes(rank, T, topo):
    src = T.cores[rank]
    later = list(range(len(T.cores) - 1, rank, -1))
    straight = [r for r in later if topo.may_write(src, T.cores[r])]
    cross = [r for r in later if r not in straight]
    if not cross:
        return straight, []
    able = [h for h in topo.cores_of(src) if h != src and T.rank_of(h) is None and topo.may_write(h, T.cores[cross[0]])]
    able.sort(key=lambda h: (topo.die(h) != topo.die(src), h))
    n = min(2, len(cross), len(able))
    eng = topo.engines(src, able[0])
    inner = [e for e in eng if e not in topo.engines(able[0], T.cores[cross[0]])]
    return straight, [(able[i], cross[i::n], inner if i else eng) for i in range(n)]


def fan(g, T, topo, core, ranks, src, dst, rsem):
    ids = []
    for r in ranks:
        rid, pid = topo.addr(T.cores[r], core)
        ids.append(DstId(rid=rid, pnc=pid))
    g.remote_dma_fused([RemoteDMATransfer(dst_ids=ids, dma_engine_mask=topo.mask(core, T.cores[ranks[0]]), remote_sem=rsem,
                                          srcs=[src], dsts=[dst for _ in ranks])], local_sem=T.sem.loc)
    return len(topo.engines(core, T.cores[ranks[0]]))


def helper(g, core, T, topo):
    for r in range(len(T.cores)):
        if core not in topo.cores_of(T.cores[r]):
            continue
        for h, ranks, eng in routes(r, T, topo)[1]:
            if h != core:
                continue
            n = 0
            g.wait_ge(T.sem.hle, len(eng))
            n += fan(g, T, topo, core, ranks, T.hle[:, :], T["V%d" % r][:, 0:64], T.sem.le)
            g.wait_ge(T.sem.hli, len(eng))
            for d in ranks:
                n += fan(g, T, topo, core, [d], T.hli[:, :], T["T%d" % r][:, :], T.sem["ar%d" % r])
            g.wait_ge(T.sem.loc, n)


def rank_program(g, core, T, topo):
    rank = T.rank_of(core)
    if rank is None:
        helper(g, core, T, topo)
        return
    op = AluOpType
    fn = ActivationFunctionType
    V, S, PE, SY = g.vector, g.scalar, g.tensor, g.sync
    queue = {"v": V, "s": S, "pe": PE, "gi": g, "sy": SY}
    cnt = {}
    seen = {}

    def need(q, toks):
        top = {}
        for sem, val in toks:
            top[sem] = max(top.get(sem, 0), val)
        for sem in top:
            if seen.get((q, sem), 0) < top[sem]:
                queue[q].wait_ge(T.sem[sem], top[sem])
                seen[(q, sem)] = top[sem]

    def done(sem, ins, n=1):
        ins.then_inc(T.sem[sem], n)
        cnt[sem] = cnt.get(sem, 0) + n
        return (sem, cnt[sem])

    def gath(q, out, win, lst, deps):
        need(q, deps)
        if q == "v":
            return done("v", V.tensor_copy(out=out, in_=win.indirect(lst)))
        return done("s", S.activation(out=out, in_=win.indirect(lst), func=fn.Copy))

    def scan(out, data0, data1, initial, op0, op1, deps):
        need("v", deps)
        return done("v", V.tensor_tensor_scan(out=out, data0=data0, data1=data1, initial=initial, op0=op0, op1=op1))

    def ts(out, in0, s1, s2, op0, op1, deps):
        need("v", deps)
        if op1 is None:
            return done("v", V.tensor_scalar(out=out, in0=in0, scalar1=s1, scalar2=None, op0=op0))
        return done("v", V.tensor_scalar(out=out, in0=in0, scalar1=s1, scalar2=s2, op0=op0, op1=op1))

    mine = T["V%d" % rank]
    straight, relays = routes(rank, T, topo)
    last = not straight and not relays
    early_rank = rank < EARLY
    ln = done("dln", SY.dma_start(out=T.xl[:, :], in_=T.ln[:, :]), 16)
    ds = done("dds", S.dma_start(out=T.xd[:, :], in_=T.ds[:, :]), 16)
    le = done("dle", SY.dma_start(out=mine[:, 0:64], in_=T.le[:, :]), 16)
    flag = {"allow_small_or_imprecise_dtypes": True}
    add = float(OFF - BIG)
    ident = {}

    def roots(i):
        ident[i] = done("gi", g.iota(T["W%d" % i][:, 0:320], [[1, 320]], -OFF, 0, **flag))

    ui = done("gi", g.iota(T.ui[:, :], [[1, 16]], 128, -1))
    ei = done("gi", g.iota(T.ei[:, :], [[1, 8], [0, 16]], 0, -1))
    bh = done("gi", g.iota(T.B[:, 0:1024 - BG], [[0, 1024 - BG]], 0, 0, **flag))
    bg = done("gi", g.iota(T.B[:, 1024 - BG:BG], [[0, 2 * BG - 1024]], 0, 0, **flag))
    roots(0)
    a1 = done("v", V.memset(T.A[:, 0:HALF], 1.0))
    uu = ts(T.uu[:, :], T.ui[:, :], 15, None, op.bitwise_and, None, [ui])
    ma = ts(T.ma[:, :], T.uu[:, :], 0.0, -8192.0, op.is_equal, op.mult, [uu])
    mb = ts(T.mb[:, :], T.uu[:, :], 1.0, float(BIG), op.is_equal, op.mult, [uu])
    ee = ts(T.ee[:, :], T.ei[:, :], 0.0, None, op.is_equal, None, [ei])
    need("v", [ma, mb])
    mtok = {16: done("v", V.tensor_tensor(out=T.mm[:, 0:16], in0=T.ma[:, :], in1=T.mb[:, :], op=op.add))}

    def widen(to):
        w = max(mtok)
        while w < to:
            n = min(w, to - w)
            need("s", [mtok[w]])
            mtok[w + n] = done("s", S.activation(out=T.mm[:, w:w + n], in_=T.mm[:, 0:n], func=fn.Copy))
            w += n

    need("s", [a1])
    a2 = done("s", S.activation(out=T.A[:, HALF:2 * HALF], in_=T.A[:, 0:HALF], func=fn.Copy))
    widen(64)
    last16 = T.mb[:, 0:1]

    def relist(src, tmp, n, deps):
        return scan(tmp, T.mm[:, 0:n], src, 0.0, op.add, op.max, deps + [mtok[min(w for w in mtok if w >= n)], mb])

    def offs(out, picked, deps):
        return ts(out, picked, last16, add, op.add, op.add, deps)

    lastf = scan(T.lastf[:, :], T.A[0:8, 16:80], T.xl[:, :], -1.0, op.add, op.add, [ln, a1])
    need("pe", [lastf, ee])
    p1 = done("pe", PE.matmul(T.ps1[:, 0:64], T.ee[:, :], T.lastf[:, :], True, True))
    need("v", [ds])
    df = done("v", V.tensor_copy(out=T.df[:, :], in_=T.xd[:, :]))
    av63 = done("v", V.memset(T.av[:, 63:64], 1.0))
    ob = ts(T.ob[:, :], T.mb[:, 0:1], add, None, op.add, None, [mb])
    need("pe", [df])
    p2 = done("pe", PE.matmul(T.ps2[:, 0:64], T.ee[:, :], T.df[:, :], True, True))
    need("s", [p2])
    avt = done("s", S.activation(out=T.av[:, 0:63], in_=T.ps2[:, 1:64], func=fn.Identity, bias=1.0, scale=-1.0))
    bvt = done("s", S.activation(out=T.bv[:, :], in_=T.ps2[:, 0:64], func=fn.Copy))
    need("s", [a2])
    first = done("s", S.activation(out=T.A[:, 15:16], in_=T.ps2[:, 0:1], func=fn.Identity, bias=1.0, scale=-1.0))
    need("s", [bh])
    b0 = done("s", S.activation(out=T.B[:, BG:1024], in_=T.B[:, 0:1024 - BG], func=fn.Copy))
    widen(512)
    t = relist(T.ps1[:, 0:64], T.lsc[:, :], 64, [p1])
    lw = ts(T.lastw[:, :], T.lsc[:, 15:64:16], last16, -float(BIG), op.add, op.add, [t])
    need("v", [lw, avt, av63, a2])
    sca = done("v", V.tensor_copy(out=T.A[:, 16:1040].indirect(T.lastw[:, 0:4]), in_=T.av[:, :]))
    need("v", [bvt, b0, bg])
    scb = done("v", V.tensor_copy(out=T.B[:, 0:1024].indirect(T.lastw[:, 0:4]), in_=T.bv[:, :]))
    h = scan(T.f16[:, :], T.A[:, 15:1039], T.B[:, :], float(319 - OFF), op.add, op.add, [sca, scb, first])
    need("s", [h])
    fcopy = done("s", S.activation(out=T.W0[:, 320:320 + SC1], in_=T.f16[:, 0:SC1], func=fn.Copy))
    need("gi", [h])
    gcopy = done("gi", g.affine_select(T.W0[:, 320 + SC1:1344], T.f16[:, SC1:1024], [[0, 1024 - SC1]], op.is_equal, 0.0, 0, 0))
    for i in (1, 2, 3):
        roots(i)
    z0 = done("gi", g.iota(T.V0[:, 64:320], [[0, 256]], 0, 0, **flag))
    relist(T.f16[:, 0:512], T.r16[:, 0:512], 512, [h])
    t = relist(T.f16[:, 512:1024], T.r16[:, 512:1024], 512, [h])
    l1 = offs(T.L1[:, :], T.r16[:, 15:1024:16], [t])
    need("v", [fcopy, gcopy, ident[0]])
    code = done("v", V.tensor_copy(out=T.W0[:, 320:1344].indirect(T.lastw[:, 0:4]), in_=T.W0[:, 0:64]))

    base = 320
    LIST = {1: T.L1, 3: T.L3, 9: T.L9, 27: T.L27}
    WIN = {k: T["W%d" % (i % 4)] for i, k in enumerate(POW)}
    made = {1: [(0, 1024, code)]}
    listed = {1: [(0, 1024, l1)]}
    readers = {}

    def after(where, a, b):
        return [x[2] for x in where if x[0] < b and a < x[1]]

    def whole(k):
        return [ident[POW.index(k) % 4]] + after(made[k], 0, 1024)

    def jump(q, a_, b_, c0, c1):
        k = a_ + b_
        i = POW.index(k)
        old = readers.get(POW[i - 4], []) if i >= 4 else []
        deps = [ident[POW.index(a_) % 4]] + after(made[a_], 0, c1) + after(listed[b_], c0, c1) + old
        t = gath(q, WIN[k][:, base + c0:base + c1], WIN[a_][:, 0:base + c1], LIST[b_][:, c0 // 16:c1 // 16], deps)
        readers.setdefault(a_, []).append(t)
        made.setdefault(k, []).append((c0, c1, t))

    def pick(k, c0, c1):
        return relist(WIN[k][:, base + c0:base + c1], T.SC[:, c0:c1], c1 - c0, after(made[k], c0, c1))

    def lists(q, k, c0, c1, toks):
        out, src = LIST[k][:, c0 // 16:c1 // 16], T.SC[:, c0 + 15:c1:16]
        if q == "v":
            t = offs(out, src, toks)
        else:
            need("s", toks + [ob])
            t = done("s", S.activation(out=out, in_=src, func=fn.Identity, bias=T.ob[:, 0:1]))
        listed.setdefault(k, []).append((c0, c1, t))

    def tail(k, lst, c0, out, deps):
        deps = deps + whole(k)
        win = WIN[k][:, :]
        a = gath("v", T.t16[:, 768:896], win, lst[:, c0:c0 + 8], deps)
        b = gath("s", T.t16[:, 896:1024], win, lst[:, c0 + 8:c0 + 16], deps)
        t = relist(T.t16[:, 768:1024], T.q16[:, 768:1024], 256, [a, b])
        return offs(out, T.q16[:, 783:1024:16], [t])

    jump("s", 1, 1, 0, 256)
    jump("v", 1, 1, 256, 512)
    jump("s", 1, 1, 512, 768)
    jump("v", 1, 1, 768, 1024)
    lt = None
    for k in (1, 3, 9):
        if k == 9 and early_rank:
            jump("s", 18, 9, XC, 1024)
            jump("v", 18, 9, 0, XC)
            t = relist(WIN[18][:, base + 768:base + 1024], T.SC[:, 768:1024], 256, after(made[18], 768, 1024))
            lt = offs(T.TA[:, :], T.SC[:, 783:1024:16], [t])
            lt = tail(27, T.TA, 0, T.TB[:, :], [lt])
            lt = tail(27, T.TB, 0, T.LF[:, 48:64], [lt])
        else:
            jump("s", 2 * k, k, XV, H)
            jump("v", 2 * k, k, 0, XV)
            jump("s", 2 * k, k, H, B1)
            jump("s", 2 * k, k, B1, 1024)
        lists("s", 3 * k, 0, H, [pick(3 * k, 0, H)])
        jump("s", 3 * k, 3 * k, 0, XY)
        t = [pick(3 * k, H, B1), pick(3 * k, B1, 1024)]
        jump("v", 3 * k, 3 * k, XY, H)
        lists("v", 3 * k, H, 1024, t)
        jump("v", 3 * k, 3 * k, H, XZ)
        jump("s", 3 * k, 3 * k, XZ, 1024)
    fb = whole(54) + after(listed[27], 0, 1024)
    if not early_rank and not last:
        lt = tail(54, T.L27, 48, T.LF[:, 48:64], fb)

    loc = 0
    for what in () if last else ("le", "list"):
        early = what == "le"
        need("gi", [le] if early else [lt])
        src = mine[:, 0:64] if early else T.LF[:, 48:64]
        calls = []
        if relays:
            calls.append((relays[0], None))
        if straight:
            calls.append((None, straight if early else straight[:1]))
        calls += [(x, None) for x in relays[1:]]
        if straight[1:] and not early:
            calls.append((None, straight[1:]))
        for relay, ranks in calls:
            if relay:
                h, _, eng = relay
                rid, pid = topo.addr(h, core)
                g.remote_dma(out_ap=T.hle[:, :] if early else T.hli[:, :], in_ap=src,
                             remote_sem=T.sem.hle if early else T.sem.hli, local_sem=T.sem.loc,
                             pid=pid, routing_id=rid, dma_engine_mask=bits(eng))
                loc += len(eng)
            else:
                dst = mine[:, 0:64] if early else T["T%d" % rank][:, :]
                loc += fan(g, T, topo, core, ranks, src, dst, T.sem.le if early else T.sem["ar%d" % rank])

    n = 1024 if last else 768
    m = n // 2
    FB = WIN[54][:, :]
    tv = gath("v", T.t16[:, 0:m], FB, T.L27[:, 0:m // 16], fb)
    ts_ = gath("s", T.t16[:, m:n], FB, T.L27[:, m // 16:n // 16], fb)
    relist(T.t16[:, 0:m], T.q16[:, 0:m], m, [tv])
    t = relist(T.t16[:, m:n], T.q16[:, m:n], m, [ts_])
    lr = offs(T.LF[:, 0:n // 16], T.q16[:, 15:n:16], [t])

    prev = [z0]
    total_le = 0
    got = []
    for k in range(rank):
        hop = [c for c in routes(k, T, topo)[1] if rank in c[1]]
        n = len(topo.engines(hop[0][0] if hop else T.cores[k], core))
        total_le += n
        got.append(("ar%d" % k, n))
    for k in range(rank):
        w, nx, lst = T["V%d" % k], T["V%d" % (k + 1)], T["T%d" % k]
        deps = prev + [("le", total_le), got[k]]
        a = gath("v", nx[:, 64:192], w[:, 0:320], lst[:, 0:8], deps)
        b = gath("s", nx[:, 192:320], w[:, 0:320], lst[:, 8:16], deps)
        prev = [a, b]

    win = mine[:, 0:320]
    deps = prev + [le, lr] + ([] if last else [lt])
    for q, issue, a, b in (("v", "sy", 0, 320), ("s", "sy", 512, 832), ("v", "sy", 320, 512), ("s", "s", 832, 1024)):
        t = gath(q, T.yb[:, a:b], win, T.LF[:, a // 16:b // 16], deps)
        need(issue, [t])
        done("dy", queue[issue].dma_start(out=T.y[:, a:b], in_=T.yb[:, a:b]), 16)
    need("sy", [(s, cnt[s]) for s in ("dy", "v", "s", "pe", "gi", "dln", "dds", "dle")])
    if loc:
        g.wait_ge(T.sem.loc, loc)
